import numpy as np, ml_dtypes
CORES = [16,17,18,19,32,33,34,35]
N = 8
BF = ml_dtypes.bfloat16
W, LN, HO, TH = 4096, 320, 4, 60
def spot(a, s, k):
    return ((a * s >> 5) + a + 37 * s + k) & (W - 1)
def parts(rng):
    return (rng.integers(0, 16, (N, 8, 16, W)), rng.integers(0, W, (N, 8, 16, LN)), rng.integers(0, 16, (N, 8, 16, LN)), rng.integers(0, 16, (N, 8, 16, LN)),
            rng.integers(0, W, (N, 8, LN)), rng.integers(0, W, (N, 8, 16)))
def pack(X, P, A, R, s, K):
    b = lambda v, n: np.ascontiguousarray(np.reshape(v, (N, 128, n))).astype(np.float32).astype(BF)
    return {"x": b(X, W), "pn": np.ascontiguousarray(P.reshape(N, 128, LN)).astype(np.int32), "a0": b(A, LN), "r0": b(R, LN),
            "s0": np.ascontiguousarray(s).astype(np.int32), "kap": np.ascontiguousarray(K.reshape(N, 128, 1)).astype(np.int32)}
def setup_inputs(rng):
    return pack(*parts(rng))
def setup_inputs_spread(rng):
    X, P, A, R, s, K = parts(rng); lg = W.bit_length() - 1
    def small(n):
        top = rng.integers(0, 16, (N, 8, 1, n)); return np.minimum((rng.random((N, 8, 16, n)) * (top + 1)).astype(np.int64), top)
    def skew(*sh):
        v = np.minimum(np.exp2(lg * rng.random(sh)).astype(np.int64) - 1, W - 1); return np.where(rng.random(sh) < 0.5, v, W - 1 - v)
    X, P, A, R, s, K = small(W), skew(N, 8, 16, LN), small(LN), small(LN), skew(N, 8, LN), skew(N, 8, 16)
    pairs = ((3, 21), (21, 3), (5, 19), (19, 5), (7, 9), (9, 7))
    for q in range(N):
        for g in range(0, 8, 2):
            u, v = pairs[int(rng.integers(0, 6))]; l = int(rng.integers(0, LN))
            s[q, g, l] = W - u; K[q, g] = (W - v - spot(P[q, g, :, l], W - u, 0)) & (W - 1)
    return pack(X, P, A, R, s, K)
def setup_inputs_ends(rng):
    e = W - 1; bit = lambda *sh: rng.integers(0, 2, sh)
    def ends(n):
        v = 15 * bit(N, 8, 16, n); return np.where(rng.random((N, 8, 1, n)) < 0.5, v[:, :, :1], v)
    X, A, R = ends(W), ends(LN), ends(LN); P, s, K = e * bit(N, 8, 16, LN), e * bit(N, 8, LN), e * bit(N, 8, 16)
    K[:, :, 15] = 0; K[:, :, 14] = e
    for l in (0, 1, 6, LN - 2, LN - 1): P[..., l] = e; s[..., l] = e
    s[..., 3] = 0; s[..., LN - 3] = 0
    lo = sorted(set(spot(a, 0, k) for a in (0, e) for k in (0, e))); hi = sorted(set(spot(a, e, k) for a in (0, e) for k in (0, e)))
    w = bit(N, 8, 1, 1); o = rng.permutation(N - 1)
    for q, far in ((N - 1, 1), (int(o[0]), 0), (int(o[1]), 1)):
        X[q][:, :, lo] = 15 * w[q]; X[q][:, :, hi] = 15 * (1 - w[q])
        A[q] = 15 * ((w[q] + (s[q][:, None, :] > 0) + far) & 1)
    c = int(o[1]); A[c, 7, :, LN - 1] = 15 - A[c, 7, :, LN - 1]
    return pack(X, P, A, R, s, K)
def setup_inputs_corners(rng):
    X, P, A, R, s, K = parts(rng); off = int(rng.integers(0, 4)); H = W // 2; row = np.arange(16)[:, None]
    for q in range(N):
        for g in range(8):
            m = (q + g + off) % 4
            if m == 0:
                c = rng.integers(0, 16, (16, 1)); X[q, g] = c; A[q, g] = c; R[q, g] = c
            elif m == 1:
                c = 15 * int(rng.integers(0, 2)); X[q, g] = c; A[q, g] = 15 - c; R[q, g] = 15 - c
                if g >= 4:
                    s[q, g] = int(rng.integers(0, 32)); P[q, g, 0] = rng.permutation(H)[:LN]
            elif m == 2:
                c = 15 * int(rng.integers(0, 2)); X[q, g, :, :H] = c; X[q, g, :, H:] = 15 - c; A[q, g] = c; R[q, g] = np.where(rng.random(LN) < 0.5, c, 15 - c)
                kind = rng.integers(0, 8, LN); kind[:8] = np.arange(8); kind[LN - 8:] = rng.permutation(8)
                rows = row + np.zeros((1, LN), np.int64)
                mk = np.stack([rows < 0, rows == 0, rows == 15, (rows == 0) | (rows == 15), rows < 15, rows == rng.integers(0, 16, (1, LN)), rows >= 0, rows == 14])
                near = mk[kind, :, np.arange(LN)].T
                site = np.where(rng.random((16, LN)) < 0.3, (H - 1) * rng.integers(0, 2, (16, LN)), rng.integers(0, H, (16, LN))) + np.where(near, 0, H)
                s[q, g] = 0; P[q, g] = (site - K[q, g][:, None]) & (W - 1)
            else:
                s[q, g] = rng.choice(np.array([0, 1, H, W - 1]), LN); K[q, g] = (W - 1) * rng.integers(0, 2, 16)
                P[q, g] = np.where(rng.random((16, LN)) < 0.4, s[q, g][None, :], (W - 1) * rng.integers(0, 2, (16, LN)))
    return pack(X, P, A, R, s, K)
def setup_inputs_crowd(rng):
    X, P, A, R, s, K = parts(rng); h = LN // 2
    P[:, 3] = P[:, 3, :1]
    P[:, ::2] = P[:, ::2, :, :1].copy(); s[:, ::2] = s[:, ::2, :1].copy()
    P[:, 1:7:2, :, h:] = P[:, 1:7:2, :, :h][..., ::-1].copy(); s[:, 1:7:2, h:] = s[:, 1:7:2, :h][..., ::-1].copy()
    P[:, 7, :, 1::2] = P[:, 7, :, ::2].copy(); s[:, 7, 1::2] = s[:, 7, ::2].copy()
    for g in (0, 6):
        A[:, g] = rng.integers(8, 16, (N, 16, LN))
        for q in range(N): X[q, g][:, spot(P[q, g, :, 0], s[q, g, 0], K[q, g])] = 0
    return pack(X, P, A, R, s, K)
def gaps(rng):
    n = np.where(rng.random((N, 8, 1, LN)) < 0.4, TH - 1, TH + rng.integers(0, 17, (N, 8, 1, LN))); n[..., 0] = TH; n[..., LN - 1] = TH - 1
    return n
def dist(rng, z, n):
    i = np.argsort(rng.random((N, 8, 16, LN)), axis=2)
    return np.abs(z - ((n + i) >> 4))
def setup_inputs_ties(rng):
    X, P, A, R, s, K = parts(rng)
    z = 15 * rng.integers(0, 2, (N, 8, 1, W)); z[:, ::2] = z[:, ::2, :, :1].copy()
    zl = 15 * rng.integers(0, 2, (N, 8, 1, LN)); zl[:, ::2] = z[:, ::2, :, :1]
    c = int(rng.integers(0, N)); b = (c - 1) % N; a = (c - 2) % N
    zc = 15 * ((np.arange(8) // 2 + int(rng.integers(0, 2))) & 1)[:, None, None]
    z[c] = zc
    for q in (a, b): z[q, ::2] = zc[::2]
    for q in (a, b, c): zl[q] = zc
    na, nr = gaps(rng), gaps(rng)
    na[b] = TH - 1; nr[b] = TH - 1; na[c] = TH - 1; na[c, :, 0, 0] = TH
    e = int(rng.integers(1, 8)); gs = rng.integers(0, 8, e); ls = 1 + rng.permutation(LN - 2)[:e]
    na[c, gs, 0, ls] = TH + rng.integers(0, 17, e)
    X[:] = z
    return pack(X, P, dist(rng, zl, na), dist(rng, zl, nr), s, K)
def check_inputs(d):
    bad = []
    for k, lo, hi in (("x", 0, 15), ("pn", 0, W - 1), ("a0", 0, 15), ("r0", 0, 15), ("s0", 0, W - 1), ("kap", 0, W - 1)):
        v = np.asarray(d[k]).astype(np.float64)
        if not np.all((v >= lo) & (v <= hi) & (v == np.floor(v))): bad.append("range of " + k)
    return bad
def reference(x, pn, a0, r0, s0, kap):
    X = x.astype(np.float32).astype(np.int64).reshape(N, 8, 16, W); P = pn.astype(np.int64).reshape(N, 8, 16, LN)
    A = a0.astype(np.float32).astype(np.int64).reshape(N, 8, 16, LN); R = r0.astype(np.float32).astype(np.int64).reshape(N, 8, 16, LN)
    s = s0.astype(np.int64); K = kap.astype(np.int64).reshape(N, 8, 16, 1)
    p = np.zeros((N, 8, LN), np.int64); ex = np.zeros((N, 8, LN), np.int64); missed = np.zeros(N, np.int64); row = np.arange(16)[:, None]
    for t in range(HO):
        last = missed; missed = np.zeros(N, np.int64)
        for r in range(N):
            q = (r + t) % N
            h = spot(P[r], s[r][:, None, :], K[q])
            v = np.take_along_axis(X[q], h.reshape(8, 1, 16 * LN), 2).reshape(8, 16, 16, LN)
            dd = np.add.reduce(np.abs(v - A[r][:, :, None, :]), axis=1)
            near = (dd < TH + (last[q] & 15)) & (row >= p[r][:, None, :]); hit = np.any(near, axis=1)
            k = np.where(hit, 15 - np.argmax(near[:, ::-1], axis=1), p[r])
            hk = np.take_along_axis(h, k[:, None, :], 1)[:, 0]
            back = ((s[r] * hk >> 5) + s[r] + 811 * t) & (W - 1)
            new = np.where((row >= p[r][:, None, :]) & (row <= k[:, None, :]), back[:, None, :], P[r])
            turn = ~hit | (k == 15); tu = turn[:, None, :]
            for g in range(8):
                m = np.flatnonzero(~hit[g]); place, first = np.unique(hk[g][m], return_index=True); lane = m[first]
                X[q, g][:, place] = (X[q, g][:, place] + A[r, g][:, lane]) >> 1
            missed[q] = np.count_nonzero(~hit)
            P[r] = np.where(tu, new[:, ::-1], new); p[r] = np.where(turn, 15 - k, k + 1); s[r] = hk; ex[r] = ex[r] ^ turn
            A[r], R[r] = np.where(tu, R[r], A[r]), np.where(tu, A[r], R[r])
    at = [(q - (HO - 1)) % N for q in range(N)]
    return {"yn": P[at].reshape(N, 128, LN).astype(np.float32), "ys": s[at].astype(np.float32), "yp": (p[at] + 16 * ex[at]).astype(np.float32),
            "yx": X.reshape(N, 128, W).astype(np.float32).astype(BF)}

@@ -1,0 +1,549 @@
+from concourse.mybir import AluOpType, ActivationFunctionType
+
+LN = 320
+RW = 16
+NC = LN // RW
+HO = 4
+SITES = 4096
+XW = SITES + 448
+SROWS = 2
+
+MB_NAMES = ["BO", "TRI", "EYE", "SH", "JJ", "TJ", "TP1", "TP2", "TJT", "NTRI", "EN", "ES1", "ES2", "WT", "NEYE",
+            "IJ", "I2K", "JI2K", "I8K", "N2I", "CONE", "D01", "D10"]
+MH_NAMES = ["I16", "JI16", "BO16", "Q00", "Q01", "Q10", "Q11", "C2080", "CM2K", "G8H"]
+
+SCRATCH = {
+    "xs": ("sbuf", [128, XW], "bfloat16"),
+    "pni": ("sbuf", [128, LN], "int32"),
+    "s0i": ("sbuf", [8, LN], "int32"),
+    "s0h": ("sbuf", [8, LN], "float16"),
+    "kpi": ("sbuf", [128, 1], "int32"),
+    "kcol": ("sbuf", [128, 1], "float32"),
+    "rin": ("sbuf", [128, LN], "bfloat16"),
+    "a2": ("sbuf", [128, 2 * LN], "bfloat16"),
+    "ad": ("sbuf", [128, RW * LN], "bfloat16"),
+    "ab": ("sbuf", [128, RW * LN], "bfloat16"),
+    "off": ("sbuf", [128, LN], "uint16"),
+    "mb": ("sbuf", [128, 128 * len(MB_NAMES)], "bfloat16"),
+    "mh": ("sbuf", [128, 128 * len(MH_NAMES)], "float16"),
+    "zz": ("sbuf", [128, 144], "bfloat16"),
+    "z8k": ("sbuf", [128, 144], "bfloat16"),
+    "zh": ("sbuf", [128, 144], "float16"),
+    "oneb": ("sbuf", [128, LN], "bfloat16"),
+    "oneh": ("sbuf", [128, LN], "float16"),
+    "ioi": ("sbuf", [128, LN], "float32"),
+    "sent": ("sbuf", [128, LN], "bfloat16"),
+    "pidx": ("sbuf", [128, 4], "int32"),
+    "cols": ("sbuf", [128, 16], "float32"),
+    "pw": ("sbuf", [128, 24], "bfloat16"),
+    "bgh": ("sbuf", [128, 8], "float16"),
+    "dum": ("sbuf", [128, NC], "float32"),
+    "m16f": ("sbuf", [128, 128], "float32"),
+    "thr": ("sbuf", [128, 1], "float32"),
+    "mi": ("sbuf", [128, 2], "int32"),
+    "cntm": ("sbuf", [128, 1], "float32"),
+    "sf": ("sbuf", [128, LN], "float32"),
+    "w2": ("sbuf", [128, LN], "float32"),
+    "mm": ("sbuf", [128, LN], "float32"),
+    "zi": ("sbuf", [128, LN], "int32"),
+    "hi": ("sbuf", [128, LN], "int32"),
+    "hc": ("sbuf", [128, LN], "float16"),
+    "th": ("sbuf", [128, LN], "float16"),
+    "near": ("sbuf", [128, LN], "bfloat16"),
+    "miss": ("sbuf", [128, LN], "bfloat16"),
+    "sgn": ("sbuf", [128, LN], "float32"),
+    "tsb": ("sbuf", [128, LN], "bfloat16"),
+    "q1": ("sbuf", [128, LN], "float32"),
+    "q2": ("sbuf", [128, LN], "int32"),
+    "bi": ("sbuf", [128, LN], "int32"),
+    "p1": ("sbuf", [128, LN], "float16"),
+    "pt": ("sbuf", [128, LN], "float16"),
+    "xsb": ("sbuf", [128, LN], "bfloat16"),
+    "xt": ("sbuf", [128, LN], "bfloat16"),
+    "gb": ("sbuf", [128, LN], "float32"),
+    "td": ("sbuf", [128, LN], "bfloat16"),
+    "hkk": ("sbuf", [128, LN], "float32"),
+    "hko": ("sbuf", [128, NC], "uint16"),
+    "v16": ("sbuf", [128, NC], "float16"),
+    "eq": ("sbuf", [128, LN], "bfloat16"),
+    "om": ("sbuf", [128, NC], "float32"),
+    "ow": ("sbuf", [128, 2 * NC], "uint16"),
+    "sm": ("sbuf", [128, LN], "float32"),
+    "val": ("sbuf", [128, LN], "int32"),
+    "yno": ("sbuf", [128, LN], "float32"),
+    "yso": ("sbuf", [8, LN], "float32"),
+    "yci": ("sbuf", [8, LN], "int32"),
+    "ycj": ("sbuf", [8, LN], "int32"),
+    "ycf": ("sbuf", [8, LN], "float32"),
+    "ypo": ("sbuf", [8, LN], "float32"),
+}
+for _t in range(HO + 1):
+    SCRATCH["si%d" % _t] = ("sbuf", [128, 3 * LN], "bfloat16")
+    SCRATCH["ai%d" % _t] = ("sbuf", [128, 2 * LN], "bfloat16")
+    SCRATCH["pi%d" % _t] = ("sbuf", [128, LN], "float16")
+    SCRATCH["ji%d" % _t] = ("sbuf", [128, LN], "float16")
+for _t in range(1, HO + 1):
+    SCRATCH["so%d" % _t] = ("sbuf", [128, 3 * LN], "bfloat16")
+    SCRATCH["ao%d" % _t] = ("sbuf", [128, 2 * LN], "bfloat16")
+    SCRATCH["po%d" % _t] = ("sbuf", [128, LN], "float16")
+    SCRATCH["jo%d" % _t] = ("sbuf", [128, 2 * LN], "float16")
+for _k in ("si4", "ai4", "pi4", "ji0", "ji4"):
+    del SCRATCH[_k]
+for _k in range(8):
+    SCRATCH["ps%d" % _k] = ("psum", [128, 512], "float32")
+
+NDMA = 16
+SEMAPHORES = (["eV", "eS", "eT", "eG", "ls"] + ["d%d" % i for i in range(NDMA)]
+              + ["r%s%d" % (k, t) for t in range(1, HO) for k in "japs"])
+
+
+def O(name, a, b, step=1, p=None):
+    return (name, a, b, step, p)
+
+
+def make_queue(g, T):
+    eng = {"v": g.vector, "s": g.scalar, "t": g.tensor, "g": g, "y": g.sync}
+    esem = {"v": "eV", "s": "eS", "t": "eT", "g": "eG"}
+    know = {q: {} for q in eng}
+    count = {}
+    snaps = {}
+    recs = {}
+
+    def learn(q, tok):
+        k = know[q]
+        if k.get(tok[0], 0) >= tok[1]:
+            return
+        eng[q].wait_ge(T.sem[tok[0]], tok[1])
+        k[tok[0]] = tok[1]
+        for s, n in snaps.get(tok, {}).items():
+            if k.get(s, 0) < n:
+                k[s] = n
+
+    def ap(o):
+        name, a, b, step, p = o
+        t = T[name]
+        if p is None:
+            return t[:, a:b] if step == 1 else t[:, a:b:step]
+        return t[0:p, a:b] if step == 1 else t[0:p, a:b:step]
+
+    def needs(q, tag, reads, writes):
+        out = []
+        for lst, w in ((reads, False), (writes, True)):
+            for o in lst:
+                ps = o[0].startswith("ps")
+                for (a, b, rw, rq, tok) in recs.get(o[0], []):
+                    if not ps and (a >= o[2] or b <= o[1]):
+                        continue
+                    if rq == tag and tag != "dma":
+                        if (rw or w) and not (w and tag == "t"):
+                            out.append(tok)
+                        continue
+                    if w or rw or ps:
+                        out.append(tok)
+        return out
+
+    def note(tag, tok, reads, writes):
+        for lst, w in ((reads, False), (writes, True)):
+            for o in lst:
+                a, b = (0, 1 << 20) if o[0].startswith("ps") else (o[1], o[2])
+                old = recs.get(o[0], [])
+                if w:
+                    old = [r for r in old if not (r[0] >= a and r[1] <= b)]
+                elif tag != "dma":
+                    old = [r for r in old if not (r[0] >= a and r[1] <= b and not r[2] and r[3] == tag)]
+                recs[o[0]] = old + [(a, b, w, tag, tok)]
+
+    def op(q, fn, reads, writes):
+        need = needs(q, q, reads, writes)
+        for tok in sorted(set(need), key=lambda x: -x[1]):
+            learn(q, tok)
+        s = esem[q]
+        count[s] = count.get(s, 0) + 1
+        fn().then_inc(T.sem[s], 1)
+        tok = (s, count[s])
+        snaps[tok] = dict(know[q])
+        note(q, tok, reads, writes)
+        return tok
+
+    ndma = [0]
+
+    def dma(q, out, in_, reads, writes):
+        for tok in set(needs(q, "dma", reads, writes)):
+            learn(q, tok)
+        s = "d%d" % ndma[0]
+        ndma[0] += 1
+        eng[q].dma_start(out, in_).then_inc(T.sem[s], 16)
+        tok = (s, 16)
+        count[s] = 16
+        snaps[tok] = dict(know[q])
+        note("dma", tok, reads, writes)
+
+    def arrive(s, n, o):
+        tok = (s, n)
+        count[s] = n
+        note("dma", tok, [], [o])
+
+    def ready(q, reads):
+        for tok in sorted(set(needs(q, "dma", reads, [])), key=lambda x: -x[1]):
+            learn(q, tok)
+
+    def finish(local):
+        for s, n in sorted(count.items()):
+            learn("g", (s, n))
+        if local:
+            g.wait_ge(T.sem.ls, local)
+
+    return ap, op, dma, arrive, ready, finish
+
+
+def rank_program(g, core, T, topo):
+    rank = T.rank_of(core)
+    if rank is None:
+        return
+    n = len(T.cores)
+    nxt, prv = T.cores[(rank + 1) % n], T.cores[(rank - 1) % n]
+    ap, op, dma, arrive, ready, finish = make_queue(g, T)
+    ALU, ACT = AluOpType, ActivationFunctionType
+    V, S, PE = g.vector, g.scalar, g.tensor
+
+    def tt(out, i0, i1, f):
+        op("v", lambda: V.tensor_tensor(ap(out), ap(i0), ap(i1), f), [i0, i1], [out])
+
+    def ts(out, i0, s1, s2, f0, f1=None):
+        cols = [x for x in (s1, s2) if isinstance(x, tuple)]
+        a1 = ap(s1) if isinstance(s1, tuple) else s1
+        a2 = ap(s2) if isinstance(s2, tuple) else s2
+        if f1 is None:
+            op("v", lambda: V.tensor_scalar(ap(out), ap(i0), a1, None, f0), [i0] + cols, [out])
+        else:
+            op("v", lambda: V.tensor_scalar(ap(out), ap(i0), a1, a2, f0, f1), [i0] + cols, [out])
+
+    def cp(out, i0):
+        op("v", lambda: V.tensor_copy(ap(out), ap(i0)), [i0], [out])
+
+    def fill(out, c):
+        op("v", lambda: V.memset(ap(out), c), [], [out])
+
+    def act(out, i0, f, bias=0.0, scale=1.0, acc=None):
+        rd = [i0] + ([bias] if isinstance(bias, tuple) else [])
+        bb = ap(bias) if isinstance(bias, tuple) else bias
+        if acc is None:
+            op("s", lambda: S.activation(ap(out), ap(i0), f, bias=bb, scale=scale), rd, [out])
+        else:
+            op("s", lambda: S.activation(ap(out), ap(i0), f, bias=bb, scale=scale, accum_out=ap(acc)), rd, [out, acc])
+
+    def mm(out, lhsT, rhs, start, stop):
+        op("t", lambda: PE.matmul(ap(out), ap(lhsT), ap(rhs), start, stop), [lhsT, rhs], [out])
+
+    def aff(out, i0, pattern, cmp_, base, cm):
+        op("g", lambda: g.affine_select(ap(out), ap(i0), pattern, cmp_, 0.0, base, cm), [i0], [out])
+
+    def gather_tt(out, win, offs, i1, f):
+        op("v", lambda: V.tensor_tensor(ap(out), ap(win).indirect(ap(offs)), ap(i1), f), [win, offs, i1], [out])
+
+    def gather_act(out, win, offs):
+        op("s", lambda: S.activation(ap(out), ap(win).indirect(ap(offs)), ACT.Copy), [win, offs], [out])
+
+    def scatter(win, offs, i0):
+        op("v", lambda: V.tensor_copy(ap(win).indirect(ap(offs)), ap(i0)), [i0, offs], [win])
+
+    sent_local = [0]
+
+    def send(dst, src, key, t):
+        ready("g", [src])
+        rid, pid, _ = topo.addr(nxt)
+        g.remote_dma(ap(dst), ap(src), T.sem["r%s%d" % (key, t)], T.sem.ls, pid, rid, topo.mask(core, nxt))
+        sent_local[0] += len(topo.engines(core, nxt))
+
+    def MB(k, r=128):
+        i = MB_NAMES.index(k)
+        return O("mb", 128 * i, 128 * i + 128)
+
+    def MH(k, p=None):
+        i = MH_NAMES.index(k)
+        return O("mh", 128 * i, 128 * i + 128, 1, p)
+
+    def Z(name, k):
+        return O(name, 15 - k, 143 - k)
+
+    def PS(k, a=0, b=LN, step=1, p=None):
+        return O("ps%d" % k, a, b, step, p)
+
+    def all_(name):
+        return O(name, 0, LN)
+
+    y = "y"
+    dma(y, ap(O("pni", 0, LN)), T.pn[:], [], [O("pni", 0, LN)])
+    dma("s", ap(O("s0i", 0, LN)), T.s0[:], [], [O("s0i", 0, LN)])
+    dma("s", ap(O("kpi", 0, 1)), T.kap[:], [], [O("kpi", 0, 1)])
+    dma(y, ap(O("ai0", 0, LN)), T.a0[:], [], [O("ai0", 0, LN)])
+    dma("s", ap(all_("rin")), T.r0[:], [], [all_("rin")])
+    dma(y, ap(O("xs", 0, SITES)), T.x[:], [], [O("xs", 0, SITES)])
+    SITE = O("xs", 0, SITES)
+    SITEW = O("xs", 0, XW)
+
+    for t in range(1, HO):
+        k = len(topo.engines(prv, core))
+        arrive("rj%d" % t, k, all_("ji%d" % t))
+        arrive("ra%d" % t, k, O("ai%d" % t, 0, 2 * LN))
+        arrive("rp%d" % t, k, all_("pi%d" % t))
+        arrive("rs%d" % t, k, O("si%d" % t, 0, 3 * LN))
+
+    fill(all_("oneb"), 1.0)
+    cp(all_("oneh"), all_("oneb"))
+    op("g", lambda: g.iota(ap(O("pidx", 0, 1)), [[0, 1]], 0, 1), [], [O("pidx", 0, 1)])
+    one = O("oneb", 0, 128)
+    one8 = O("oneb", 0, 128, 1, 8)
+    tmp8 = O("near", 0, 128, 1, 8)
+    aff(tmp8, one8, [[1, 128]], ALU.is_ge, 0, -16)
+    aff(tmp8, tmp8, [[-1, 128]], ALU.is_ge, 15, 16)
+    tb = O("near", 128, 256)
+    aff(tb, one, [[-16, 8], [0, 16]], ALU.is_ge, 0, 1)
+    aff(MB("BO"), tb, [[16, 8], [0, 16]], ALU.is_ge, 15, -1)
+    aff(MB("EYE"), MB("BO"), [[-1, 128]], ALU.is_equal, 0, 1)
+    aff(MB("D01"), one, [[1, 128]], ALU.is_equal, -16, -1)
+    aff(MB("D10"), one, [[1, 128]], ALU.is_equal, 16, -1)
+    aff(MB("TRI"), MB("BO"), [[-1, 128]], ALU.is_ge, 0, 1)
+    aff(MB("JJ"), one, [[-16, 8], [1, 16]], ALU.is_equal, -15, 1)
+    aff(MB("TJ"), MB("BO"), [[16, 8], [-1, 16]], ALU.is_ge, 14, -1)
+    aff(MB("SH"), MB("BO"), [[1, 128]], ALU.is_equal, -1, -1)
+    op("g", lambda: g.iota(ap(O("dum", 0, NC)), [[16, NC]], 2048, 1, allow_small_or_imprecise_dtypes=True), [], [O("dum", 0, NC)])
+    op("g", lambda: g.iota(ap(all_("ioi")), [[0, NC], [1, RW]], 0, 0, allow_small_or_imprecise_dtypes=True), [], [all_("ioi")])
+
+    def col(i):
+        return O("cols", i, i + 1)
+    ts(O("pidx", 1, 2), O("pidx", 0, 1), 15, None, ALU.bitwise_and)
+    ts(O("pidx", 2, 3), O("pidx", 0, 1), 4, 1, ALU.arith_shift_right, ALU.bitwise_and)
+    cp(col(0), O("pidx", 1, 2))
+    cp(col(2), O("pidx", 2, 3))
+    ts(col(1), col(0), 15.0, None, ALU.is_equal)
+    ts(col(3), col(2), -1.0, 1.0, ALU.mult, ALU.add)
+    ts(col(4), col(1), -101.0, 1.0, ALU.mult, ALU.add)
+    ts(col(5), col(0), 1.0, None, ALU.add)
+    ts(col(6), col(0), -2.0, 14.0, ALU.mult, ALU.add)
+    ts(col(7), col(0), 0.0, None, ALU.is_equal)
+    fill(MH("C2080"), 16.25)
+    cp(MH("G8H", 8), tmp8)
+    ts(all_("pi0"), all_("pni"), -2048.0, None, ALU.add)
+    ts(O("s0h", 0, LN, 1, 8), O("s0i", 0, LN, 1, 8), -2048.0, None, ALU.add)
+    ts(O("kcol", 0, 1), O("kpi", 0, 1), 32.0, -37888.0 - 80.0 * 131072.0, ALU.mult, ALU.add)
+
+    def prep(t):
+        if t == 0:
+            mm(PS(0), MH("G8H", 8), O("s0h", 0, LN, 1, 8), True, False)
+        else:
+            mm(PS(0), MH("BO16"), all_("ji%d" % t), True, False)
+        mm(PS(0), MH("C2080"), all_("oneh"), False, True)
+        act(PS(1), PS(0), ACT.Identity, O("kcol", 0, 1), 3232.0)
+        tt(all_("mm"), all_("pi%d" % t), PS(0), ALU.mult)
+        act(all_("sf"), PS(0), ACT.Copy, -32.0)
+        act(all_("w2"), PS(0), ACT.Copy, -32.0 * 2080.0 + 32.0 * 811.0 * t - 8388608.0, 2080.0)
+        tt(all_("zi"), all_("mm"), PS(1), ALU.add)
+        ts(all_("hi"), all_("zi"), 5, SITES - 1, ALU.arith_shift_right, ALU.bitwise_and)
+        ts(all_("hc"), all_("hi"), -2048.0, None, ALU.add)
+        for b in range(NC // 2):
+            o, i = O("th", b, LN, NC // 2), O("hc", 32 * b, 32 * b + 32)
+            op("v", lambda: V.transpose(ap(o), ap(i)), [i], [o])
+        for x in range(2):
+            for y2 in range(2):
+                mm(PS(2, x, LN, 2), MH("Q%d%d" % (x, y2)), O("th", 160 * y2, 160 * y2 + 160), y2 == 0, y2 == 1)
+        ts(all_("off"), PS(2), 2048.0, None, ALU.add)
+        mm(PS(3), MH("I16"), all_("hc"), True, True)
+        mm(PS(4), MH("I16"), all_("hc"), True, False)
+        act(O("a2", 0, LN), O("ai%d" % t, 0, LN), ACT.Copy)
+        act(O("a2", LN, 2 * LN), O("ai%d" % t, 0, LN), ACT.Copy)
+
+    ts(MH("I16"), MB("EYE"), 1.0, None, ALU.mult)
+    ts(MH("Q00"), MB("EYE"), col(3), None, ALU.mult)
+    ts(MH("Q11"), MB("EYE"), col(2), None, ALU.mult)
+    ts(MH("Q01"), MB("D01"), col(3), None, ALU.mult)
+    ts(MH("Q10"), MB("D10"), col(2), None, ALU.mult)
+    prep(0)
+    ts(MB("NEYE"), MB("EYE"), -1.0, None, ALU.mult)
+    fill(O("zz", 0, 144), 0.0)
+    cp(O("zz", 15, 143, 16), O("mb", 0, 128, 16))
+    ts(O("si0", 0, LN), all_("oneb"), col(1), None, ALU.mult)
+    ts(O("si0", LN, 2 * LN), all_("oneb"), col(1), None, ALU.mult)
+    fill(O("si0", 2 * LN, 3 * LN), 0.0)
+    ts(MB("TP1"), MB("TRI"), 256.0, None, ALU.mult)
+    tt(MB("TJT"), MB("TJ"), MB("TRI"), ALU.subtract)
+    ts(MB("TP2"), MB("TJT"), 256.0, None, ALU.mult)
+    ts(MB("ES1"), MB("SH"), -1.0, None, ALU.mult)
+    tt(MB("ES2"), MB("SH"), MB("JJ"), ALU.subtract)
+    ts(MB("NTRI"), MB("TRI"), -1.0, None, ALU.mult)
+    ts(MB("I8K"), MB("EYE"), 4.0, None, ALU.mult)
+    ts(MB("EN"), MB("TRI"), 3.0, None, ALU.mult)
+    tt(MB("EN"), MB("EN"), MB("I8K"), ALU.subtract)
+    ts(MB("I8K"), MB("EYE"), 8192.0, None, ALU.mult)
+    ts(MB("WT"), MB("BO"), col(4), None, ALU.mult)
+    fill(MB("CONE"), 1.0 / 128.0)
+    fill(MH("CM2K"), -16.0)
+    ts(MH("BO16"), MB("BO"), 1.0, None, ALU.mult)
+    tt(MB("IJ"), MB("EYE"), MB("JJ"), ALU.subtract)
+    ts(MB("I2K"), MB("EYE"), 2048.0, None, ALU.mult)
+    ts(MB("JI2K"), MB("IJ"), -2048.0, None, ALU.mult)
+    ts(MH("JI16"), MB("IJ"), -1.0, None, ALU.mult)
+    ts(MB("N2I"), MB("EYE"), -2.0, None, ALU.mult)
+    ts(O("z8k", 0, 144), O("zz", 0, 144), 8192.0, None, ALU.mult)
+    cp(O("zh", 0, 144), O("zz", 0, 144))
+    ts(all_("sent"), all_("ioi"), col(0), 8192.0, ALU.is_le, ALU.mult)
+    b8 = O("mb", 0, 128, 16)
+    ts(O("pw", 0, 8), b8, col(5), None, ALU.mult)
+    ts(O("pw", 8, 16), b8, col(6), None, ALU.mult)
+    ts(O("pw", 16, 24), b8, col(7), None, ALU.mult)
+    cp(O("bgh", 0, 8), b8)
+    fill(O("m16f", 0, 128), 1.0 / 16.0)
+    fill(O("thr", 0, 1), 60.0)
+    tt(O("ai0", LN, 2 * LN), all_("rin"), O("ai0", 0, LN), ALU.subtract)
+
+    VROWS = RW - SROWS
+    for t in range(HO):
+        last = t == HO - 1
+        si, ai, pi = "si%d" % t, "ai%d" % t, "pi%d" % t
+        so, ao, po, jo = "so%d" % (t + 1), "ao%d" % (t + 1), "po%d" % (t + 1), "jo%d" % (t + 1)
+        osel, oselT = O(si, 0, LN), O(si, LN, 2 * LN)
+        gather_act(O("ad", VROWS * LN, RW * LN), SITE, O("off", VROWS * NC, RW * NC))
+        k = 0
+        first = [True]
+
+        def add_rows(r0, r1):
+            for r in range(r0, r1):
+                mm(PS(5), Z("zz", r), O("ab", r * LN, r * LN + LN), first[0], r == VROWS - 1)
+                first[0] = False
+        steps = []
+        while k < VROWS:
+            w = 2 if k + 2 < VROWS else 1
+            steps.append((k, k + w))
+            k += w
+        for j, (r0, r1) in enumerate(steps):
+            gather_tt(O("ad", r0 * LN, r1 * LN), SITE, O("off", r0 * NC, r1 * NC), O("a2", 0, (r1 - r0) * LN), ALU.subtract)
+            act(O("ab", r0 * LN, r1 * LN), O("ad", r0 * LN, r1 * LN), ACT.Abs)
+            if j == 1:
+                for r in range(VROWS, RW):
+                    bank = 6 + r - VROWS
+                    mm(PS(bank), MB("EYE"), O("ad", r * LN, r * LN + LN), True, False)
+                    mm(PS(bank), MB("NEYE"), O("a2", 0, LN), False, True)
+            add_rows(r0, r1)
+            if j == 2:
+                for r in range(VROWS, RW):
+                    act(O("ab", r * LN, r * LN + LN), PS(6 + r - VROWS), ACT.Abs)
+                add_rows(VROWS, RW)
+            if j == 3:
+                mm(PS(5), MB("TP1"), osel, False, False)
+                mm(PS(5), MB("TP2"), oselT, False, False)
+                mm(PS(6), MB("ES1"), osel, True, False)
+                mm(PS(6), MB("ES2"), oselT, False, False)
+                mm(PS(1), MB("CONE"), all_("oneb"), True, False)
+                mm(PS(1), MB("TRI"), osel, False, False)
+                mm(PS(1), MB("TJT"), oselT, False, False)
+        ts(all_("near"), PS(5), O("thr", 0, 1), None, ALU.is_lt)
+        mm(PS(6), MB("EN"), all_("near"), False, True)
+        mm(PS(7), MB("WT"), all_("near"), True, True)
+        mm(PS(4), MB("I8K"), all_("near"), False, True)
+        if not last:
+            mm(PS(0), MB("BO"), all_("near"), True, True)
+        sel = O(so, 0, LN)
+        ts(sel, PS(6), -0.5, None, ALU.is_lt)
+        act(all_("sgn"), PS(7), ACT.Sign, -0.5)
+        M, M2 = O(jo, 0, LN), O(jo, LN, 2 * LN)
+        tt(M, sel, PS(3), ALU.mult)
+        mm(PS(1), MB("NTRI"), sel, False, True)
+        mm(PS(5), MH("BO16"), M, True, True)
+        tt(M2, sel, PS(4), ALU.mult)
+        act(PS(2), all_("sgn"), ACT.Relu, 0.0, -1.0)
+        act(all_("tsb"), all_("sgn"), ACT.Relu, 0.0, -1.0)
+        act(all_("xsb"), PS(1), ACT.Copy)
+        act(all_("hkk"), PS(5), ACT.Copy)
+        if not last:
+            act(all_("miss"), PS(0), ACT.Relu, 1.0, -1.0, O("cntm", 0, 1))
+            send(all_("ji%d" % (t + 1)), M, "j", t + 1)
+
+        def names():
+            tt(all_("p1"), all_(pi), PS(1), ALU.mult)
+            tt(all_("q1"), all_("sf"), PS(5), ALU.mult)
+            tt(all_("q2"), all_("q1"), all_("w2"), ALU.add)
+            tt(all_("pt"), all_("p1"), PS(2), ALU.mult)
+            tt(all_("xt"), all_("tsb"), PS(1), ALU.mult)
+            mm(PS(6), MB("CONE"), all_("oneb"), True, False)
+            mm(PS(6), MB("NEYE"), all_("xsb"), False, False)
+            mm(PS(6), MB("IJ"), all_("xt"), False, True)
+            mm(PS(7), MH("I16"), all_("p1"), True, False)
+            mm(PS(7), MH("JI16"), all_("pt"), False, False)
+            mm(PS(7), MB("I2K"), all_("xsb"), False, False)
+            if not last:
+                mm(PS(7), MH("CM2K"), all_("oneh"), False, False)
+            mm(PS(7), MB("JI2K"), all_("xt"), False, True)
+            ts(all_("bi"), all_("q2"), 5, SITES - 1, ALU.arith_shift_right, ALU.bitwise_and)
+            tt(all_("gb"), all_("bi"), PS(6), ALU.mult)
+            tt(all_("yno") if last else all_(po), all_("gb"), PS(7), ALU.add)
+
+        def turned():
+            tt(O(so, LN, 2 * LN), sel, PS(2), ALU.mult)
+            tt(O(so, 2 * LN, 3 * LN), O(si, 2 * LN, 3 * LN), PS(2), ALU.add)
+
+        def find_writers1():
+            for i in range(RW):
+                mm(PS(3, 0, 2 * NC), Z("zh", i), O(jo, i, 2 * LN, RW), i == 0, i == RW - 1)
+            mm(PS(4), MB("EYE"), all_("sent"), True, False)
+
+        def find_writers2():
+            ts(O("hko", 0, NC), PS(3, 0, NC), 2048.0, None, ALU.add)
+            cp(O("v16", 0, NC), PS(3, NC, 2 * NC))
+            for i in range(RW):
+                mm(PS(4, i, LN, RW), MH("I16"), O("v16", 0, NC), False, i == RW - 1)
+            mm(PS(3, 0, NC), MH("I16"), O("v16", 0, NC), True, False)
+            gather_tt(all_("sm"), SITE, O("hko", 0, NC), O("a2", 0, LN), ALU.add)
+            ts(all_("val"), all_("sm"), 0.5, -0.25, ALU.mult, ALU.add)
+
+        def write_sites():
+            tt(all_("eq"), all_("hkk"), PS(4), ALU.is_equal)
+            for i in range(RW):
+                mm(PS(3, 0, NC), Z("z8k", i), O("eq", i, LN, RW), False, i == RW - 1)
+            tt(O("om", 0, NC), PS(3, 0, NC), O("dum", 0, NC), ALU.min)
+            ts(O("ow", 0, 2 * NC, 2), O("om", 0, NC), 2048.0, None, ALU.add)
+            for c in range(NC - 1, -1, -1):
+                scatter(SITEW, O("ow", 2 * c, 2 * c + 1), O("val", RW * c, RW * c + RW))
+
+        find_writers1()
+        if last:
+            find_writers2()
+            write_sites()
+            for h in range(2):
+                dma("y" if h == 0 else "s", T.yx[:, 2048 * h:2048 * h + 2048], ap(O("xs", 2048 * h, 2048 * h + 2048)),
+                    [O("xs", 2048 * h, 2048 * h + 2048)], [])
+            names()
+            dma("y", T.yn[:], ap(all_("yno")), [all_("yno")], [])
+            turned()
+            r8 = lambda name: O(name, 0, LN, 1, 8)
+            mm(PS(0, 0, LN, 1, 8), O("bgh", 0, 8), M, True, True)
+            act(r8("yso"), PS(0, 0, LN, 1, 8), ACT.Copy, 2048.0)
+            dma("s", T.ys[:], ap(r8("yso")), [r8("yso")], [])
+            mm(PS(4, 0, LN, 1, 8), O("pw", 16, 24), O(so, 2 * LN, 3 * LN), True, True)
+            cp(r8("yci"), PS(4, 0, LN, 1, 8))
+            mm(PS(6, 0, LN, 1, 8), O("pw", 0, 8), sel, True, False)
+            mm(PS(6, 0, LN, 1, 8), O("pw", 8, 16), O(so, LN, 2 * LN), False, True)
+            ts(r8("ycj"), r8("yci"), 1, None, ALU.bitwise_and)
+            ts(r8("ycf"), r8("ycj"), 16.0, None, ALU.mult)
+            tt(r8("ypo"), r8("ycf"), PS(6, 0, LN, 1, 8), ALU.add)
+            dma("y", T.yp[:], ap(r8("ypo")), [r8("ypo")], [])
+        else:
+            names()
+            send(all_("pi%d" % (t + 1)), all_(po), "p", t + 1)
+            tt(all_("td"), O(ai, LN, 2 * LN), PS(2), ALU.mult)
+            mm(PS(0), MB("EYE"), O(ai, 0, LN), True, False)
+            mm(PS(0), MB("EYE"), all_("td"), False, True)
+            mm(PS(1), MB("EYE"), O(ai, LN, 2 * LN), True, False)
+            mm(PS(1), MB("N2I"), all_("td"), False, True)
+            act(O(ao, 0, LN), PS(0), ACT.Copy)
+            act(O(ao, LN, 2 * LN), PS(1), ACT.Copy)
+            send(O("ai%d" % (t + 1), 0, 2 * LN), O(ao, 0, 2 * LN), "a", t + 1)
+            turned()
+            send(O("si%d" % (t + 1), 0, 3 * LN), O(so, 0, 3 * LN), "s", t + 1)
+            find_writers2()
+            mm(PS(5, 0, 1), O("m16f", 0, 128), O("cntm", 0, 1), True, True)
+            cp(O("mi", 0, 1), PS(5, 0, 1))
+            ts(O("mi", 1, 2), O("mi", 0, 1), 15, None, ALU.bitwise_and)
+            ts(O("thr", 0, 1), O("mi", 1, 2), 60.0, None, ALU.add)
+            write_sites()
+            prep(t + 1)
+    finish(sent_local[0])

@@ -3,14 +3,15 @@ from concourse.mybir import AluOpType, ActivationFunctionType
 LN = 320
 RW = 16
 NC = LN // RW
+NP = NC // 2
 HO = 4
 SITES = 4096
 XW = SITES + 448
 SROWS = 2
 
 MB_NAMES = ["BO", "TRI", "EYE", "SH", "JJ", "TJ", "TP1", "TP2", "TJT", "NTRI", "EN", "ES1", "ES2", "WT", "NEYE",
-            "IJ", "I2K", "JI2K", "I8K", "N2I", "CONE", "D01", "D10"]
-MH_NAMES = ["I16", "JI16", "BO16", "Q00", "Q01", "Q10", "Q11", "C2080", "CM2K", "G8H"]
+            "IJ", "JI", "I8K", "N2I", "D01", "D10", "Q00", "Q01", "Q10", "Q11", "C2080", "C2K",
+            "G8", "TM1", "TM2"]
 
 SCRATCH = {
     "xs": ("sbuf", [128, XW], "bfloat16"),
@@ -25,18 +26,15 @@ SCRATCH = {
     "ab": ("sbuf", [128, RW * LN], "bfloat16"),
     "off": ("sbuf", [128, LN], "uint16"),
     "mb": ("sbuf", [128, 128 * len(MB_NAMES)], "bfloat16"),
-    "mh": ("sbuf", [128, 128 * len(MH_NAMES)], "float16"),
     "zz": ("sbuf", [128, 144], "bfloat16"),
     "z8k": ("sbuf", [128, 144], "bfloat16"),
-    "zh": ("sbuf", [128, 144], "float16"),
     "oneb": ("sbuf", [128, LN], "bfloat16"),
-    "oneh": ("sbuf", [128, LN], "float16"),
+    "neg": ("sbuf", [128, NP], "bfloat16"),
     "ioi": ("sbuf", [128, LN], "float32"),
-    "sent": ("sbuf", [128, LN], "bfloat16"),
+    "sent": ("sbuf", [128, LN + LN // 2], "bfloat16"),
     "pidx": ("sbuf", [128, 4], "int32"),
     "cols": ("sbuf", [128, 16], "float32"),
-    "pw": ("sbuf", [128, 24], "bfloat16"),
-    "bgh": ("sbuf", [128, 8], "float16"),
+    "pw": ("sbuf", [128, 32], "bfloat16"),
     "dum": ("sbuf", [128, NC], "float32"),
     "m16f": ("sbuf", [128, 128], "float32"),
     "thr": ("sbuf", [128, 1], "float32"),
@@ -44,7 +42,7 @@ SCRATCH = {
     "cntm": ("sbuf", [128, 1], "float32"),
     "sf": ("sbuf", [128, LN], "float32"),
     "w2": ("sbuf", [128, LN], "float32"),
-    "mm": ("sbuf", [128, LN], "float32"),
+    "wk": ("sbuf", [128, LN], "float32"),
     "zi": ("sbuf", [128, LN], "int32"),
     "hi": ("sbuf", [128, LN], "int32"),
     "hc": ("sbuf", [128, LN], "float16"),
@@ -52,8 +50,6 @@ SCRATCH = {
     "near": ("sbuf", [128, LN], "bfloat16"),
     "miss": ("sbuf", [128, LN], "bfloat16"),
     "sgn": ("sbuf", [128, LN], "float32"),
-    "tsb": ("sbuf", [128, LN], "bfloat16"),
-    "q1": ("sbuf", [128, LN], "float32"),
     "q2": ("sbuf", [128, LN], "int32"),
     "bi": ("sbuf", [128, LN], "int32"),
     "p1": ("sbuf", [128, LN], "float16"),
@@ -62,13 +58,14 @@ SCRATCH = {
     "xt": ("sbuf", [128, LN], "bfloat16"),
     "gb": ("sbuf", [128, LN], "float32"),
     "td": ("sbuf", [128, LN], "bfloat16"),
-    "hkk": ("sbuf", [128, LN], "float32"),
+    "hkk": ("sbuf", [128, LN + LN // 2], "float32"),
     "hko": ("sbuf", [128, NC], "uint16"),
-    "v16": ("sbuf", [128, NC], "float16"),
-    "eq": ("sbuf", [128, LN], "bfloat16"),
+    "v16": ("sbuf", [128, NC + NP], "float16"),
+    "eq": ("sbuf", [128, LN + LN // 2], "bfloat16"),
     "om": ("sbuf", [128, NC], "float32"),
-    "ow": ("sbuf", [128, 2 * NC], "uint16"),
-    "sm": ("sbuf", [128, LN], "float32"),
+    "o2": ("sbuf", [128, NP], "float32"),
+    "ow": ("sbuf", [128, NC], "uint16"),
+    "sm": ("sbuf", [128, LN], "bfloat16"),
     "val": ("sbuf", [128, LN], "int32"),
     "yno": ("sbuf", [128, LN], "float32"),
     "yso": ("sbuf", [8, LN], "float32"),
@@ -78,23 +75,23 @@ SCRATCH = {
     "ypo": ("sbuf", [8, LN], "float32"),
 }
 for _t in range(HO + 1):
-    SCRATCH["si%d" % _t] = ("sbuf", [128, 3 * LN], "bfloat16")
+    SCRATCH["si%d" % _t] = ("sbuf", [128, 4 * LN], "bfloat16")
     SCRATCH["ai%d" % _t] = ("sbuf", [128, 2 * LN], "bfloat16")
     SCRATCH["pi%d" % _t] = ("sbuf", [128, LN], "float16")
     SCRATCH["ji%d" % _t] = ("sbuf", [128, LN], "float16")
 for _t in range(1, HO + 1):
-    SCRATCH["so%d" % _t] = ("sbuf", [128, 3 * LN], "bfloat16")
+    SCRATCH["so%d" % _t] = ("sbuf", [128, 2 * LN], "bfloat16")
     SCRATCH["ao%d" % _t] = ("sbuf", [128, 2 * LN], "bfloat16")
     SCRATCH["po%d" % _t] = ("sbuf", [128, LN], "float16")
     SCRATCH["jo%d" % _t] = ("sbuf", [128, 2 * LN], "float16")
 for _k in ("si4", "ai4", "pi4", "ji0", "ji4"):
     del SCRATCH[_k]
 for _k in range(8):
-    SCRATCH["ps%d" % _k] = ("psum", [128, 512], "float32")
+    SCRATCH["ps%d" % _k] = ("psum", [128, 16, 32] if _k == 5 else [128, 512], "float32")
 
 NDMA = 16
 SEMAPHORES = (["eV", "eS", "eT", "eG", "ls"] + ["d%d" % i for i in range(NDMA)]
-              + ["r%s%d" % (k, t) for t in range(1, HO) for k in "japs"])
+              + ["r%s%d" % (k, t) for t in range(1, HO) for k in "japshd"])
 
 
 def O(name, a, b, step=1, p=None):
@@ -122,6 +119,8 @@ def make_queue(g, T):
     def ap(o):
         name, a, b, step, p = o
         t = T[name]
+        if name == "ps5":
+            return t[:, 0:NP, :] if p is None else t[:, 0:NP, p[0]:p[1]]
         if p is None:
             return t[:, a:b] if step == 1 else t[:, a:b:step]
         return t[0:p, a:b] if step == 1 else t[0:p, a:b:step]
@@ -131,8 +130,10 @@ def make_queue(g, T):
         for lst, w in ((reads, False), (writes, True)):
             for o in lst:
                 ps = o[0].startswith("ps")
-                for (a, b, rw, rq, tok) in recs.get(o[0], []):
+                for (a, b, step, rw, rq, tok) in recs.get(o[0], []):
                     if not ps and (a >= o[2] or b <= o[1]):
+                        continue
+                    if not ps and step == o[3] and step > 1 and (a - o[1]) % step:
                         continue
                     if rq == tag and tag != "dma":
                         if (rw or w) and not (w and tag == "t"):
@@ -145,13 +146,14 @@ def make_queue(g, T):
     def note(tag, tok, reads, writes):
         for lst, w in ((reads, False), (writes, True)):
             for o in lst:
-                a, b = (0, 1 << 20) if o[0].startswith("ps") else (o[1], o[2])
+                ps = o[0].startswith("ps")
+                a, b, st = (0, 1 << 20, 1) if ps else (o[1], o[2], o[3])
                 old = recs.get(o[0], [])
                 if w:
-                    old = [r for r in old if not (r[0] >= a and r[1] <= b)]
+                    old = [r for r in old if not (r[0] >= a and r[1] <= b and st == 1)]
                 elif tag != "dma":
-                    old = [r for r in old if not (r[0] >= a and r[1] <= b and not r[2] and r[3] == tag)]
-                recs[o[0]] = old + [(a, b, w, tag, tok)]
+                    old = [r for r in old if not (r[0] >= a and r[1] <= b and st == 1 and not r[3] and r[4] == tag)]
+                recs[o[0]] = old + [(a, b, st, w, tag, tok)]
 
     def op(q, fn, reads, writes):
         need = needs(q, q, reads, writes)
@@ -225,18 +227,25 @@ def rank_program(g, core, T, topo):
         op("v", lambda: V.memset(ap(out), c), [], [out])
 
     def act(out, i0, f, bias=0.0, scale=1.0, acc=None):
-        rd = [i0] + ([bias] if isinstance(bias, tuple) else [])
+        rd = [i0] + [x for x in (bias, scale) if isinstance(x, tuple)]
         bb = ap(bias) if isinstance(bias, tuple) else bias
+        ss = ap(scale) if isinstance(scale, tuple) else scale
         if acc is None:
-            op("s", lambda: S.activation(ap(out), ap(i0), f, bias=bb, scale=scale), rd, [out])
+            op("s", lambda: S.activation(ap(out), ap(i0), f, bias=bb, scale=ss), rd, [out])
         else:
-            op("s", lambda: S.activation(ap(out), ap(i0), f, bias=bb, scale=scale, accum_out=ap(acc)), rd, [out, acc])
+            op("s", lambda: S.activation(ap(out), ap(i0), f, bias=bb, scale=ss, accum_out=ap(acc)), rd, [out, acc])
+
+    def scaled(out, i0, c):
+        act(out, i0, ACT.Identity, 0.0, c)
 
     def mm(out, lhsT, rhs, start, stop):
         op("t", lambda: PE.matmul(ap(out), ap(lhsT), ap(rhs), start, stop), [lhsT, rhs], [out])
 
     def aff(out, i0, pattern, cmp_, base, cm):
         op("g", lambda: g.affine_select(ap(out), ap(i0), pattern, cmp_, 0.0, base, cm), [i0], [out])
+
+    def iota(out, pattern, base, cm):
+        op("g", lambda: g.iota(ap(out), pattern, base, cm, allow_small_or_imprecise_dtypes=True), [], [out])
 
     def gather_tt(out, win, offs, i1, f):
         op("v", lambda: V.tensor_tensor(ap(out), ap(win).indirect(ap(offs)), ap(i1), f), [win, offs, i1], [out])
@@ -255,13 +264,9 @@ def rank_program(g, core, T, topo):
         g.remote_dma(ap(dst), ap(src), T.sem["r%s%d" % (key, t)], T.sem.ls, pid, rid, topo.mask(core, nxt))
         sent_local[0] += len(topo.engines(core, nxt))
 
-    def MB(k, r=128):
+    def MB(k, p=None):
         i = MB_NAMES.index(k)
-        return O("mb", 128 * i, 128 * i + 128)
-
-    def MH(k, p=None):
-        i = MH_NAMES.index(k)
-        return O("mh", 128 * i, 128 * i + 128, 1, p)
+        return O("mb", 128 * i, 128 * i + 128, 1, p)
 
     def Z(name, k):
         return O(name, 15 - k, 143 - k)
@@ -272,43 +277,46 @@ def rank_program(g, core, T, topo):
     def all_(name):
         return O(name, 0, LN)
 
-    y = "y"
-    dma(y, ap(O("pni", 0, LN)), T.pn[:], [], [O("pni", 0, LN)])
-    dma("s", ap(O("s0i", 0, LN)), T.s0[:], [], [O("s0i", 0, LN)])
-    dma("s", ap(O("kpi", 0, 1)), T.kap[:], [], [O("kpi", 0, 1)])
-    dma(y, ap(O("ai0", 0, LN)), T.a0[:], [], [O("ai0", 0, LN)])
-    dma("s", ap(all_("rin")), T.r0[:], [], [all_("rin")])
-    dma(y, ap(O("xs", 0, SITES)), T.x[:], [], [O("xs", 0, SITES)])
     SITE = O("xs", 0, SITES)
     SITEW = O("xs", 0, XW)
+    half = SITES // 2
+
+    dma("y", ap(all_("pni")), T.pn[:], [], [all_("pni")])
+    dma("s", ap(all_("s0i")), T.s0[:], [], [all_("s0i")])
+    dma("s", ap(O("kpi", 0, 1)), T.kap[:], [], [O("kpi", 0, 1)])
+    dma("y", ap(O("ai0", 0, LN)), T.a0[:], [], [O("ai0", 0, LN)])
+    dma("y", ap(O("xs", 0, half)), T.x[:, 0:half], [], [O("xs", 0, half)])
+    dma("s", ap(O("xs", half, SITES)), T.x[:, half:SITES], [], [O("xs", half, SITES)])
+    dma("y", ap(all_("rin")), T.r0[:], [], [all_("rin")])
 
     for t in range(1, HO):
         k = len(topo.engines(prv, core))
         arrive("rj%d" % t, k, all_("ji%d" % t))
-        arrive("ra%d" % t, k, O("ai%d" % t, 0, 2 * LN))
+        arrive("ra%d" % t, k, O("ai%d" % t, 0, LN))
+        arrive("rd%d" % t, k, O("ai%d" % t, LN, 2 * LN))
         arrive("rp%d" % t, k, all_("pi%d" % t))
-        arrive("rs%d" % t, k, O("si%d" % t, 0, 3 * LN))
+        arrive("rs%d" % t, k, O("si%d" % t, 0, 2 * LN))
+        if t > 1:
+            arrive("rh%d" % t, k, O("si%d" % t, 2 * LN, (t + 1) * LN))
 
-    fill(all_("oneb"), 1.0)
-    cp(all_("oneh"), all_("oneb"))
     op("g", lambda: g.iota(ap(O("pidx", 0, 1)), [[0, 1]], 0, 1), [], [O("pidx", 0, 1)])
+    fill(all_("oneb"), 1.0)
+    fill(MB("C2080"), 16.25)
     one = O("oneb", 0, 128)
     one8 = O("oneb", 0, 128, 1, 8)
-    tmp8 = O("near", 0, 128, 1, 8)
-    aff(tmp8, one8, [[1, 128]], ALU.is_ge, 0, -16)
-    aff(tmp8, tmp8, [[-1, 128]], ALU.is_ge, 15, 16)
-    tb = O("near", 128, 256)
-    aff(tb, one, [[-16, 8], [0, 16]], ALU.is_ge, 0, 1)
-    aff(MB("BO"), tb, [[16, 8], [0, 16]], ALU.is_ge, 15, -1)
-    aff(MB("EYE"), MB("BO"), [[-1, 128]], ALU.is_equal, 0, 1)
+    aff(MB("TM1", 8), one8, [[1, 128]], ALU.is_ge, 0, -16)
+    aff(MB("G8", 8), MB("TM1", 8), [[-1, 128]], ALU.is_ge, 15, 16)
+    aff(MB("EYE"), one, [[-1, 128]], ALU.is_equal, 0, 1)
     aff(MB("D01"), one, [[1, 128]], ALU.is_equal, -16, -1)
     aff(MB("D10"), one, [[1, 128]], ALU.is_equal, 16, -1)
+    aff(MB("TM2"), one, [[-16, 8], [0, 16]], ALU.is_ge, 0, 1)
+    aff(MB("BO"), MB("TM2"), [[16, 8], [0, 16]], ALU.is_ge, 15, -1)
     aff(MB("TRI"), MB("BO"), [[-1, 128]], ALU.is_ge, 0, 1)
-    aff(MB("JJ"), one, [[-16, 8], [1, 16]], ALU.is_equal, -15, 1)
     aff(MB("TJ"), MB("BO"), [[16, 8], [-1, 16]], ALU.is_ge, 14, -1)
+    aff(MB("JJ"), one, [[-16, 8], [1, 16]], ALU.is_equal, -15, 1)
     aff(MB("SH"), MB("BO"), [[1, 128]], ALU.is_equal, -1, -1)
-    op("g", lambda: g.iota(ap(O("dum", 0, NC)), [[16, NC]], 2048, 1, allow_small_or_imprecise_dtypes=True), [], [O("dum", 0, NC)])
-    op("g", lambda: g.iota(ap(all_("ioi")), [[0, NC], [1, RW]], 0, 0, allow_small_or_imprecise_dtypes=True), [], [all_("ioi")])
+    iota(O("dum", 0, NC), [[16, NC]], 2048, 1)
+    iota(all_("ioi"), [[0, NC], [1, RW]], 0, 0)
 
     def col(i):
         return O("cols", i, i + 1)
@@ -316,85 +324,90 @@ def rank_program(g, core, T, topo):
     ts(O("pidx", 2, 3), O("pidx", 0, 1), 4, 1, ALU.arith_shift_right, ALU.bitwise_and)
     cp(col(0), O("pidx", 1, 2))
     cp(col(2), O("pidx", 2, 3))
-    ts(col(1), col(0), 15.0, None, ALU.is_equal)
     ts(col(3), col(2), -1.0, 1.0, ALU.mult, ALU.add)
-    ts(col(4), col(1), -101.0, 1.0, ALU.mult, ALU.add)
-    ts(col(5), col(0), 1.0, None, ALU.add)
-    ts(col(6), col(0), -2.0, 14.0, ALU.mult, ALU.add)
-    ts(col(7), col(0), 0.0, None, ALU.is_equal)
-    fill(MH("C2080"), 16.25)
-    cp(MH("G8H", 8), tmp8)
-    ts(all_("pi0"), all_("pni"), -2048.0, None, ALU.add)
     ts(O("s0h", 0, LN, 1, 8), O("s0i", 0, LN, 1, 8), -2048.0, None, ALU.add)
     ts(O("kcol", 0, 1), O("kpi", 0, 1), 32.0, -37888.0 - 80.0 * 131072.0, ALU.mult, ALU.add)
+    ts(all_("pi0"), all_("pni"), -2048.0, None, ALU.add)
 
-    def prep(t):
+    def prep_site(t):
         if t == 0:
-            mm(PS(0), MH("G8H", 8), O("s0h", 0, LN, 1, 8), True, False)
+            mm(PS(0), MB("G8", 8), O("s0h", 0, LN, 1, 8), True, False)
         else:
-            mm(PS(0), MH("BO16"), all_("ji%d" % t), True, False)
-        mm(PS(0), MH("C2080"), all_("oneh"), False, True)
-        act(PS(1), PS(0), ACT.Identity, O("kcol", 0, 1), 3232.0)
-        tt(all_("mm"), all_("pi%d" % t), PS(0), ALU.mult)
+            mm(PS(0), MB("BO"), all_("ji%d" % t), True, False)
+        mm(PS(0), MB("C2080"), all_("oneb"), False, True)
+        act(all_("wk"), PS(0), ACT.Identity, O("kcol", 0, 1), 3232.0)
+
+    def prep_lists(t, between=lambda: None):
+        tt(PS(6), all_("pi%d" % t), PS(0), ALU.mult)
+        between()
         act(all_("sf"), PS(0), ACT.Copy, -32.0)
         act(all_("w2"), PS(0), ACT.Copy, -32.0 * 2080.0 + 32.0 * 811.0 * t - 8388608.0, 2080.0)
-        tt(all_("zi"), all_("mm"), PS(1), ALU.add)
+        tt(all_("zi"), all_("wk"), PS(6), ALU.add)
+        between()
         ts(all_("hi"), all_("zi"), 5, SITES - 1, ALU.arith_shift_right, ALU.bitwise_and)
+        between()
         ts(all_("hc"), all_("hi"), -2048.0, None, ALU.add)
-        for b in range(NC // 2):
-            o, i = O("th", b, LN, NC // 2), O("hc", 32 * b, 32 * b + 32)
+        between()
+        for b in range(NP):
+            o, i = O("th", b, LN, NP), O("hc", 32 * b, 32 * b + 32)
             op("v", lambda: V.transpose(ap(o), ap(i)), [i], [o])
         for x in range(2):
             for y2 in range(2):
-                mm(PS(2, x, LN, 2), MH("Q%d%d" % (x, y2)), O("th", 160 * y2, 160 * y2 + 160), y2 == 0, y2 == 1)
+                mm(PS(2, x, LN, 2), MB("Q%d%d" % (x, y2)), O("th", 160 * y2, 160 * y2 + 160), y2 == 0, y2 == 1)
+        mm(PS(3), MB("EYE"), all_("hc"), True, True)
+        mm(PS(4), MB("EYE"), all_("hc"), True, False)
+
+    def prep_rest(t):
         ts(all_("off"), PS(2), 2048.0, None, ALU.add)
-        mm(PS(3), MH("I16"), all_("hc"), True, True)
-        mm(PS(4), MH("I16"), all_("hc"), True, False)
         act(O("a2", 0, LN), O("ai%d" % t, 0, LN), ACT.Copy)
         act(O("a2", LN, 2 * LN), O("ai%d" % t, 0, LN), ACT.Copy)
 
-    ts(MH("I16"), MB("EYE"), 1.0, None, ALU.mult)
-    ts(MH("Q00"), MB("EYE"), col(3), None, ALU.mult)
-    ts(MH("Q11"), MB("EYE"), col(2), None, ALU.mult)
-    ts(MH("Q01"), MB("D01"), col(3), None, ALU.mult)
-    ts(MH("Q10"), MB("D10"), col(2), None, ALU.mult)
-    prep(0)
-    ts(MB("NEYE"), MB("EYE"), -1.0, None, ALU.mult)
+    scaled(MB("Q00"), MB("EYE"), col(3))
+    scaled(MB("Q11"), MB("EYE"), col(2))
+    scaled(MB("Q01"), MB("D01"), col(3))
+    scaled(MB("Q10"), MB("D10"), col(2))
+    prep_site(0)
+    prep_lists(0)
+    ts(col(1), col(0), 15.0, None, ALU.is_equal)
+    ts(col(5), col(0), 1.0, None, ALU.add)
+    ts(col(6), col(0), -2.0, 14.0, ALU.mult, ALU.add)
+    ts(col(7), col(0), 0.0, None, ALU.is_equal)
     fill(O("zz", 0, 144), 0.0)
-    cp(O("zz", 15, 143, 16), O("mb", 0, 128, 16))
+    fill(MB("C2K"), 16.0)
+    fill(O("thr", 0, 1), 60.0)
+    fill(O("m16f", 0, 128), 1.0 / 16.0)
+    fill(O("neg", 0, NP), -4096.0)
+    fill(O("sent", LN, LN + LN // 2), 0.0)
+    ts(col(4), col(1), -101.0, 1.0, ALU.mult, ALU.add)
     ts(O("si0", 0, LN), all_("oneb"), col(1), None, ALU.mult)
     ts(O("si0", LN, 2 * LN), all_("oneb"), col(1), None, ALU.mult)
-    fill(O("si0", 2 * LN, 3 * LN), 0.0)
-    ts(MB("TP1"), MB("TRI"), 256.0, None, ALU.mult)
+    cp(O("zz", 15, 143, 16), O("mb", 0, 128, 16))
     tt(MB("TJT"), MB("TJ"), MB("TRI"), ALU.subtract)
-    ts(MB("TP2"), MB("TJT"), 256.0, None, ALU.mult)
-    ts(MB("ES1"), MB("SH"), -1.0, None, ALU.mult)
+    scaled(MB("NEYE"), MB("EYE"), -1.0)
+    scaled(MB("TM1"), MB("TRI"), 3.0)
+    scaled(MB("TM2"), MB("EYE"), 4.0)
+    scaled(MB("I8K"), MB("EYE"), 8192.0)
+    scaled(MB("TP1"), MB("TRI"), 4096.0)
+    scaled(MB("NTRI"), MB("TRI"), -4096.0)
+    prep_rest(0)
+    scaled(MB("ES1"), MB("SH"), -1.0)
+    scaled(MB("TP2"), MB("TJT"), 4096.0)
     tt(MB("ES2"), MB("SH"), MB("JJ"), ALU.subtract)
-    ts(MB("NTRI"), MB("TRI"), -1.0, None, ALU.mult)
-    ts(MB("I8K"), MB("EYE"), 4.0, None, ALU.mult)
-    ts(MB("EN"), MB("TRI"), 3.0, None, ALU.mult)
-    tt(MB("EN"), MB("EN"), MB("I8K"), ALU.subtract)
-    ts(MB("I8K"), MB("EYE"), 8192.0, None, ALU.mult)
-    ts(MB("WT"), MB("BO"), col(4), None, ALU.mult)
-    fill(MB("CONE"), 1.0 / 128.0)
-    fill(MH("CM2K"), -16.0)
-    ts(MH("BO16"), MB("BO"), 1.0, None, ALU.mult)
     tt(MB("IJ"), MB("EYE"), MB("JJ"), ALU.subtract)
-    ts(MB("I2K"), MB("EYE"), 2048.0, None, ALU.mult)
-    ts(MB("JI2K"), MB("IJ"), -2048.0, None, ALU.mult)
-    ts(MH("JI16"), MB("IJ"), -1.0, None, ALU.mult)
-    ts(MB("N2I"), MB("EYE"), -2.0, None, ALU.mult)
-    ts(O("z8k", 0, 144), O("zz", 0, 144), 8192.0, None, ALU.mult)
-    cp(O("zh", 0, 144), O("zz", 0, 144))
+    tt(MB("EN"), MB("TM1"), MB("TM2"), ALU.subtract)
     ts(all_("sent"), all_("ioi"), col(0), 8192.0, ALU.is_le, ALU.mult)
-    b8 = O("mb", 0, 128, 16)
-    ts(O("pw", 0, 8), b8, col(5), None, ALU.mult)
-    ts(O("pw", 8, 16), b8, col(6), None, ALU.mult)
-    ts(O("pw", 16, 24), b8, col(7), None, ALU.mult)
-    cp(O("bgh", 0, 8), b8)
-    fill(O("m16f", 0, 128), 1.0 / 16.0)
-    fill(O("thr", 0, 1), 60.0)
     tt(O("ai0", LN, 2 * LN), all_("rin"), O("ai0", 0, LN), ALU.subtract)
+    scaled(MB("WT"), MB("BO"), col(4))
+
+    def late_constants():
+        scaled(MB("JI"), MB("IJ"), -1.0)
+        scaled(MB("N2I"), MB("EYE"), -2.0)
+        scaled(O("z8k", 0, 144), O("zz", 0, 144), 8192.0)
+        b8 = O("mb", 0, 128, 16)
+        scaled(O("pw", 0, 8), b8, col(5))
+        scaled(O("pw", 8, 16), b8, col(6))
+        scaled(O("pw", 16, 24), b8, col(7))
+        scaled(O("pw", 24, 32), b8, 1.0)
 
     VROWS = RW - SROWS
     for t in range(HO):
@@ -402,23 +415,21 @@ def rank_program(g, core, T, topo):
         si, ai, pi = "si%d" % t, "ai%d" % t, "pi%d" % t
         so, ao, po, jo = "so%d" % (t + 1), "ao%d" % (t + 1), "po%d" % (t + 1), "jo%d" % (t + 1)
         osel, oselT = O(si, 0, LN), O(si, LN, 2 * LN)
+        mm(PS(5), MB("TP1"), osel, True, False)
+        mm(PS(5), MB("TP2"), oselT, False, False)
         gather_act(O("ad", VROWS * LN, RW * LN), SITE, O("off", VROWS * NC, RW * NC))
-        k = 0
-        first = [True]
 
         def add_rows(r0, r1):
             for r in range(r0, r1):
-                mm(PS(5), Z("zz", r), O("ab", r * LN, r * LN + LN), first[0], r == VROWS - 1)
-                first[0] = False
-        steps = []
-        while k < VROWS:
-            w = 2 if k + 2 < VROWS else 1
-            steps.append((k, k + w))
-            k += w
+                mm(PS(5), Z("zz", r), O("ab", r * LN, r * LN + LN), False, r == VROWS - 1)
+        steps = [(k, k + 2) for k in range(0, VROWS - 2, 2)] + [(VROWS - 2, VROWS - 1), (VROWS - 1, VROWS)]
         for j, (r0, r1) in enumerate(steps):
             gather_tt(O("ad", r0 * LN, r1 * LN), SITE, O("off", r0 * NC, r1 * NC), O("a2", 0, (r1 - r0) * LN), ALU.subtract)
             act(O("ab", r0 * LN, r1 * LN), O("ad", r0 * LN, r1 * LN), ACT.Abs)
-            if j == 1:
+            if j == 0:
+                mm(PS(1), MB("C2K"), all_("oneb"), True, False)
+                mm(PS(1), MB("TP1"), osel, False, False)
+                mm(PS(1), MB("TP2"), oselT, False, False)
                 for r in range(VROWS, RW):
                     bank = 6 + r - VROWS
                     mm(PS(bank), MB("EYE"), O("ad", r * LN, r * LN + LN), True, False)
@@ -428,122 +439,188 @@ def rank_program(g, core, T, topo):
                 for r in range(VROWS, RW):
                     act(O("ab", r * LN, r * LN + LN), PS(6 + r - VROWS), ACT.Abs)
                 add_rows(VROWS, RW)
-            if j == 3:
-                mm(PS(5), MB("TP1"), osel, False, False)
-                mm(PS(5), MB("TP2"), oselT, False, False)
                 mm(PS(6), MB("ES1"), osel, True, False)
                 mm(PS(6), MB("ES2"), oselT, False, False)
-                mm(PS(1), MB("CONE"), all_("oneb"), True, False)
-                mm(PS(1), MB("TRI"), osel, False, False)
-                mm(PS(1), MB("TJT"), oselT, False, False)
+        if t == 0:
+            late_constants()
+        sel = O(so, 0, LN)
+        M, M2 = O(jo, 0, LN), O(jo, LN, 2 * LN)
         ts(all_("near"), PS(5), O("thr", 0, 1), None, ALU.is_lt)
         mm(PS(6), MB("EN"), all_("near"), False, True)
         mm(PS(7), MB("WT"), all_("near"), True, True)
         mm(PS(4), MB("I8K"), all_("near"), False, True)
-        if not last:
-            mm(PS(0), MB("BO"), all_("near"), True, True)
-        sel = O(so, 0, LN)
         ts(sel, PS(6), -0.5, None, ALU.is_lt)
         act(all_("sgn"), PS(7), ACT.Sign, -0.5)
-        M, M2 = O(jo, 0, LN), O(jo, LN, 2 * LN)
+        act(PS(2), all_("sgn"), ACT.Relu, 0.0, -1.0)
         tt(M, sel, PS(3), ALU.mult)
         mm(PS(1), MB("NTRI"), sel, False, True)
-        mm(PS(5), MH("BO16"), M, True, True)
-        tt(M2, sel, PS(4), ALU.mult)
-        act(PS(2), all_("sgn"), ACT.Relu, 0.0, -1.0)
-        act(all_("tsb"), all_("sgn"), ACT.Relu, 0.0, -1.0)
-        act(all_("xsb"), PS(1), ACT.Copy)
-        act(all_("hkk"), PS(5), ACT.Copy)
+        mm(PS(5), MB("BO"), M, True, True)
         if not last:
-            act(all_("miss"), PS(0), ACT.Relu, 1.0, -1.0, O("cntm", 0, 1))
             send(all_("ji%d" % (t + 1)), M, "j", t + 1)
 
-        def names():
-            tt(all_("p1"), all_(pi), PS(1), ALU.mult)
-            tt(all_("q1"), all_("sf"), PS(5), ALU.mult)
-            tt(all_("q2"), all_("q1"), all_("w2"), ALU.add)
+        def v_keep():
+            tt(all_("p1"), all_(pi), PS(1), ALU.min)
+            act(all_("xsb"), PS(1), ACT.Copy, -0.5, 1.0 / 4096.0)
+
+        def v_m2():
+            tt(M2, sel, PS(4), ALU.mult)
+            for i in range(RW):
+                mm(PS(3, 0, 2 * NC), Z("zz", i), O(jo, i, 2 * LN, RW), i == 0, i == RW - 1)
+
+        def v_sites():
+            cp(O("v16", 0, NC), PS(3, NC, 2 * NC))
+            cp(O("v16", NC, NC + NP), PS(3, NC, 2 * NC, 2))
+            ts(O("hko", 0, NC), PS(3, 0, NC), 2048.0, None, ALU.add)
+
+        def pe_rep():
+            mm(PS(4, 0, LN + LN // 2), MB("EYE"), O("sent", 0, LN + LN // 2), True, False)
+            for i in range(RW):
+                mm(PS(4, i, LN + LN // 2, RW), MB("EYE"), O("v16", 0, NC + NP), False, i == RW - 1)
+
+        def s_hkk():
+            act(all_("hkk"), PS(5), ACT.Copy)
+            act(O("hkk", LN, LN + LN // 2), PS(5, 0, LN, 1, (16, 32)), ACT.Copy)
+
+        def s_new():
+            gather_act(all_("sm"), SITE, O("hko", 0, NC))
+
+        def pe_new():
+            mm(PS(5), MB("EYE"), all_("sm"), True, False)
+            mm(PS(5), MB("EYE"), O("a2", 0, LN), False, True)
+
+        def v_val():
+            ts(all_("val"), PS(5), 0.5, -0.25, ALU.mult, ALU.add)
+
+        def v_eq():
+            tt(O("eq", 0, LN + LN // 2), O("hkk", 0, LN + LN // 2), PS(4, 0, LN + LN // 2), ALU.is_equal)
+
+        def pe_dup():
+            for i in range(RW):
+                mm(PS(3, 0, NC + NP), Z("z8k", i), O("eq", i, LN + LN // 2, RW), i == 0, False)
+            mm(PS(3, 0, NC), MB("EYE"), O("v16", 0, NC), False, False)
+            mm(PS(3, NC, NC + NP), MB("EYE"), O("neg", 0, NP), False, True)
+
+        def v_places():
+            tt(O("om", 0, NC), PS(3, 0, NC), O("dum", 0, NC), ALU.min)
+            tt(O("o2", 0, NP), PS(3, NC, NC + NP), O("dum", 1, NC, 2), ALU.min)
+            v_val()
+            tt(O("om", 1, NC, 2), O("om", 1, NC, 2), O("o2", 0, NP), ALU.max)
+            ts(O("ow", 0, NC), O("om", 0, NC), 2048.0, None, ALU.add)
+
+        def v_scatter(c0, c1):
+            for c in range(c0, c1, -1):
+                scatter(SITEW, O("ow", 2 * c, 2 * c + 2), O("val", 2 * RW * c, 2 * RW * c + 2 * RW))
+
+        def pe_names1():
+            mm(PS(6), MB("NEYE"), all_("xsb"), True, False)
+            mm(PS(7), MB("EYE"), all_("p1"), True, False)
+            if last:
+                mm(PS(7), MB("C2K"), all_("oneb"), False, False)
+
+        def v_turn_v():
+            tt(all_("xt"), all_("xsb"), PS(2), ALU.mult)
             tt(all_("pt"), all_("p1"), PS(2), ALU.mult)
-            tt(all_("xt"), all_("tsb"), PS(1), ALU.mult)
-            mm(PS(6), MB("CONE"), all_("oneb"), True, False)
-            mm(PS(6), MB("NEYE"), all_("xsb"), False, False)
+
+        def pe_names2():
             mm(PS(6), MB("IJ"), all_("xt"), False, True)
-            mm(PS(7), MH("I16"), all_("p1"), True, False)
-            mm(PS(7), MH("JI16"), all_("pt"), False, False)
-            mm(PS(7), MB("I2K"), all_("xsb"), False, False)
-            if not last:
-                mm(PS(7), MH("CM2K"), all_("oneh"), False, False)
-            mm(PS(7), MB("JI2K"), all_("xt"), False, True)
+            mm(PS(7), MB("JI"), all_("pt"), False, True)
+
+        def v_b1():
+            tt(PS(0), all_("sf"), PS(5), ALU.mult)
+
+        def v_b2():
+            tt(all_("q2"), all_("w2"), PS(0), ALU.add)
             ts(all_("bi"), all_("q2"), 5, SITES - 1, ALU.arith_shift_right, ALU.bitwise_and)
+
+        def v_names():
             tt(all_("gb"), all_("bi"), PS(6), ALU.mult)
             tt(all_("yno") if last else all_(po), all_("gb"), PS(7), ALU.add)
 
-        def turned():
+        def v_turned():
             tt(O(so, LN, 2 * LN), sel, PS(2), ALU.mult)
-            tt(O(so, 2 * LN, 3 * LN), O(si, 2 * LN, 3 * LN), PS(2), ALU.add)
 
-        def find_writers1():
-            for i in range(RW):
-                mm(PS(3, 0, 2 * NC), Z("zh", i), O(jo, i, 2 * LN, RW), i == 0, i == RW - 1)
-            mm(PS(4), MB("EYE"), all_("sent"), True, False)
-
-        def find_writers2():
-            ts(O("hko", 0, NC), PS(3, 0, NC), 2048.0, None, ALU.add)
-            cp(O("v16", 0, NC), PS(3, NC, 2 * NC))
-            for i in range(RW):
-                mm(PS(4, i, LN, RW), MH("I16"), O("v16", 0, NC), False, i == RW - 1)
-            mm(PS(3, 0, NC), MH("I16"), O("v16", 0, NC), True, False)
-            gather_tt(all_("sm"), SITE, O("hko", 0, NC), O("a2", 0, LN), ALU.add)
-            ts(all_("val"), all_("sm"), 0.5, -0.25, ALU.mult, ALU.add)
-
-        def write_sites():
-            tt(all_("eq"), all_("hkk"), PS(4), ALU.is_equal)
-            for i in range(RW):
-                mm(PS(3, 0, NC), Z("z8k", i), O("eq", i, LN, RW), False, i == RW - 1)
-            tt(O("om", 0, NC), PS(3, 0, NC), O("dum", 0, NC), ALU.min)
-            ts(O("ow", 0, 2 * NC, 2), O("om", 0, NC), 2048.0, None, ALU.add)
-            for c in range(NC - 1, -1, -1):
-                scatter(SITEW, O("ow", 2 * c, 2 * c + 1), O("val", RW * c, RW * c + RW))
-
-        find_writers1()
         if last:
-            find_writers2()
-            write_sites()
-            for h in range(2):
-                dma("y" if h == 0 else "s", T.yx[:, 2048 * h:2048 * h + 2048], ap(O("xs", 2048 * h, 2048 * h + 2048)),
-                    [O("xs", 2048 * h, 2048 * h + 2048)], [])
-            names()
-            dma("y", T.yn[:], ap(all_("yno")), [all_("yno")], [])
-            turned()
             r8 = lambda name: O(name, 0, LN, 1, 8)
-            mm(PS(0, 0, LN, 1, 8), O("bgh", 0, 8), M, True, True)
+            v_m2()
+            v_b1()
+            s_hkk()
+            v_keep()
+            v_sites()
+            pe_rep()
+            s_new()
+            v_b2()
+            v_eq()
+            pe_new()
+            pe_dup()
+            v_turn_v()
+            mm(PS(0, 0, LN, 1, 8), O("pw", 24, 32), M, True, True)
             act(r8("yso"), PS(0, 0, LN, 1, 8), ACT.Copy, 2048.0)
-            dma("s", T.ys[:], ap(r8("yso")), [r8("yso")], [])
-            mm(PS(4, 0, LN, 1, 8), O("pw", 16, 24), O(so, 2 * LN, 3 * LN), True, True)
+            dma("y", T.ys[:], ap(r8("yso")), [r8("yso")], [])
+            v_places()
+            v_scatter(NP - 1, -1)
+            dma("y", T.yx[:, 0:half], ap(O("xs", 0, half)), [O("xs", 0, half)], [])
+            dma("s", T.yx[:, half:SITES], ap(O("xs", half, SITES)), [O("xs", half, SITES)], [])
+            pe_names1()
+            pe_names2()
+            v_names()
+            dma("y", T.yn[:], ap(all_("yno")), [all_("yno")], [])
+            v_turned()
+            mm(PS(4, 0, LN, 1, 8), O("pw", 24, 32), O(so, LN, 2 * LN), True, False)
+            for h in range(HO - 1):
+                mm(PS(4, 0, LN, 1, 8), O("pw", 24, 32), O(si, (h + 1) * LN, (h + 2) * LN), False, h == HO - 2)
             cp(r8("yci"), PS(4, 0, LN, 1, 8))
             mm(PS(6, 0, LN, 1, 8), O("pw", 0, 8), sel, True, False)
             mm(PS(6, 0, LN, 1, 8), O("pw", 8, 16), O(so, LN, 2 * LN), False, True)
             ts(r8("ycj"), r8("yci"), 1, None, ALU.bitwise_and)
             ts(r8("ycf"), r8("ycj"), 16.0, None, ALU.mult)
             tt(r8("ypo"), r8("ycf"), PS(6, 0, LN, 1, 8), ALU.add)
-            dma("y", T.yp[:], ap(r8("ypo")), [r8("ypo")], [])
+            dma("s", T.yp[:], ap(r8("ypo")), [r8("ypo")], [])
         else:
-            names()
+            v_keep()
+            v_m2()
+            pe_names1()
+            v_b1()
+            s_hkk()
+            v_turn_v()
+            pe_names2()
+            v_b2()
+            v_sites()
+            pe_rep()
+            s_new()
+            v_names()
             send(all_("pi%d" % (t + 1)), all_(po), "p", t + 1)
             tt(all_("td"), O(ai, LN, 2 * LN), PS(2), ALU.mult)
             mm(PS(0), MB("EYE"), O(ai, 0, LN), True, False)
             mm(PS(0), MB("EYE"), all_("td"), False, True)
-            mm(PS(1), MB("EYE"), O(ai, LN, 2 * LN), True, False)
-            mm(PS(1), MB("N2I"), all_("td"), False, True)
             act(O(ao, 0, LN), PS(0), ACT.Copy)
-            act(O(ao, LN, 2 * LN), PS(1), ACT.Copy)
-            send(O("ai%d" % (t + 1), 0, 2 * LN), O(ao, 0, 2 * LN), "a", t + 1)
-            turned()
-            send(O("si%d" % (t + 1), 0, 3 * LN), O(so, 0, 3 * LN), "s", t + 1)
-            find_writers2()
-            mm(PS(5, 0, 1), O("m16f", 0, 128), O("cntm", 0, 1), True, True)
-            cp(O("mi", 0, 1), PS(5, 0, 1))
+            send(O("ai%d" % (t + 1), 0, LN), O(ao, 0, LN), "a", t + 1)
+            mm(PS(6), MB("BO"), all_("near"), True, True)
+            act(all_("miss"), PS(6), ACT.Relu, 1.0, -1.0, O("cntm", 0, 1))
+            v_eq()
+            pe_dup()
+            v_turned()
+            mm(PS(7, 0, 1), O("m16f", 0, 128), O("cntm", 0, 1), True, True)
+            send(O("si%d" % (t + 1), 0, 2 * LN), O(so, 0, 2 * LN), "s", t + 1)
+            pe_new()
+            cp(O("mi", 0, 1), PS(7, 0, 1))
             ts(O("mi", 1, 2), O("mi", 0, 1), 15, None, ALU.bitwise_and)
             ts(O("thr", 0, 1), O("mi", 1, 2), 60.0, None, ALU.add)
-            write_sites()
-            prep(t + 1)
+            mm(PS(1), MB("EYE"), O(ai, LN, 2 * LN), True, False)
+            mm(PS(1), MB("N2I"), all_("td"), False, True)
+            act(O(ao, LN, 2 * LN), PS(1), ACT.Copy)
+            send(O("ai%d" % (t + 1), LN, 2 * LN), O(ao, LN, 2 * LN), "d", t + 1)
+            if t:
+                send(O("si%d" % (t + 1), 2 * LN, (t + 2) * LN), O(si, LN, (t + 1) * LN), "h", t + 1)
+            v_places()
+            prep_site(t + 1)
+            c = [NP - 1]
+
+            def one_scatter():
+                v_scatter(c[0], c[0] - 1)
+                c[0] -= 1
+            for h in range(3):
+                one_scatter()
+            prep_lists(t + 1, one_scatter)
+            v_scatter(c[0], -1)
+            prep_rest(t + 1)
     finish(sent_local[0])

@@ -10,7 +10,7 @@ XW = SITES + 448
 SROWS = 2
 
 MB_NAMES = ["BO", "TRI", "EYE", "SH", "JJ", "TJ", "TP1", "TP2", "TJT", "NTRI", "EN", "ES1", "ES2", "WT", "NEYE",
-            "IJ", "JI", "I8K", "N2I", "D01", "D10", "Q00", "Q01", "Q10", "Q11", "C2080", "C2K",
+            "JI", "I64", "N2I", "CX", "D01", "D10", "Q00", "Q01", "Q10", "Q11", "C2080", "C2K",
             "G8", "TM1", "TM2"]
 
 SCRATCH = {
@@ -47,15 +47,13 @@ SCRATCH = {
     "hi": ("sbuf", [128, LN], "int32"),
     "hc": ("sbuf", [128, LN], "float16"),
     "th": ("sbuf", [128, LN], "float16"),
-    "near": ("sbuf", [128, LN], "bfloat16"),
     "miss": ("sbuf", [128, LN], "bfloat16"),
     "sgn": ("sbuf", [128, LN], "float32"),
     "q2": ("sbuf", [128, LN], "int32"),
     "bi": ("sbuf", [128, LN], "int32"),
     "p1": ("sbuf", [128, LN], "float16"),
     "pt": ("sbuf", [128, LN], "float16"),
-    "xsb": ("sbuf", [128, LN], "bfloat16"),
-    "xt": ("sbuf", [128, LN], "bfloat16"),
+    "gsb": ("sbuf", [128, LN], "bfloat16"),
     "gb": ("sbuf", [128, LN], "float32"),
     "td": ("sbuf", [128, LN], "bfloat16"),
     "hkk": ("sbuf", [128, LN + LN // 2], "float32"),
@@ -66,7 +64,9 @@ SCRATCH = {
     "o2": ("sbuf", [128, NP], "float32"),
     "ow": ("sbuf", [128, NC], "uint16"),
     "sm": ("sbuf", [128, LN], "bfloat16"),
-    "val": ("sbuf", [128, LN], "int32"),
+    "va": ("sbuf", [128, LN], "bfloat16"),
+    "val": ("sbuf", [128, LN], "bfloat16"),
+    "h8": ("sbuf", [128, NC], "float16"),
     "yno": ("sbuf", [128, LN], "float32"),
     "yso": ("sbuf", [8, LN], "float32"),
     "yci": ("sbuf", [8, LN], "int32"),
@@ -325,6 +325,19 @@ def rank_program(g, core, T, topo):
     cp(col(0), O("pidx", 1, 2))
     cp(col(2), O("pidx", 2, 3))
     ts(col(3), col(2), -1.0, 1.0, ALU.mult, ALU.add)
+    ts(col(1), col(0), 15.0, None, ALU.is_equal)
+    ts(col(5), col(0), 1.0, None, ALU.add)
+    ts(col(6), col(0), -2.0, 14.0, ALU.mult, ALU.add)
+    fill(O("zz", 0, 144), 0.0)
+    fill(MB("CX"), (8192.0 - 2112.0) / 128.0)
+    fill(MB("C2K"), 16.0)
+    fill(O("thr", 0, 1), 60.0)
+    fill(O("m16f", 0, 128), 1.0 / 16.0)
+    fill(O("neg", 0, NP), -4096.0)
+    fill(O("sent", LN, LN + LN // 2), 0.0)
+    ts(col(4), col(1), -101.0, 1.0, ALU.mult, ALU.add)
+    ts(O("si0", 0, LN), all_("oneb"), col(1), None, ALU.mult)
+    ts(O("si0", LN, 2 * LN), all_("oneb"), col(1), None, ALU.mult)
     ts(O("s0h", 0, LN, 1, 8), O("s0i", 0, LN, 1, 8), -2048.0, None, ALU.add)
     ts(O("kcol", 0, 1), O("kpi", 0, 1), 32.0, -37888.0 - 80.0 * 131072.0, ALU.mult, ALU.add)
     ts(all_("pi0"), all_("pni"), -2048.0, None, ALU.add)
@@ -355,7 +368,6 @@ def rank_program(g, core, T, topo):
             for y2 in range(2):
                 mm(PS(2, x, LN, 2), MB("Q%d%d" % (x, y2)), O("th", 160 * y2, 160 * y2 + 160), y2 == 0, y2 == 1)
         mm(PS(3), MB("EYE"), all_("hc"), True, True)
-        mm(PS(4), MB("EYE"), all_("hc"), True, False)
 
     def prep_rest(t):
         ts(all_("off"), PS(2), 2048.0, None, ALU.add)
@@ -368,46 +380,30 @@ def rank_program(g, core, T, topo):
     scaled(MB("Q10"), MB("D10"), col(2))
     prep_site(0)
     prep_lists(0)
-    ts(col(1), col(0), 15.0, None, ALU.is_equal)
-    ts(col(5), col(0), 1.0, None, ALU.add)
-    ts(col(6), col(0), -2.0, 14.0, ALU.mult, ALU.add)
-    ts(col(7), col(0), 0.0, None, ALU.is_equal)
-    fill(O("zz", 0, 144), 0.0)
-    fill(MB("C2K"), 16.0)
-    fill(O("thr", 0, 1), 60.0)
-    fill(O("m16f", 0, 128), 1.0 / 16.0)
-    fill(O("neg", 0, NP), -4096.0)
-    fill(O("sent", LN, LN + LN // 2), 0.0)
-    ts(col(4), col(1), -101.0, 1.0, ALU.mult, ALU.add)
-    ts(O("si0", 0, LN), all_("oneb"), col(1), None, ALU.mult)
-    ts(O("si0", LN, 2 * LN), all_("oneb"), col(1), None, ALU.mult)
     cp(O("zz", 15, 143, 16), O("mb", 0, 128, 16))
     tt(MB("TJT"), MB("TJ"), MB("TRI"), ALU.subtract)
     scaled(MB("NEYE"), MB("EYE"), -1.0)
     scaled(MB("TM1"), MB("TRI"), 3.0)
     scaled(MB("TM2"), MB("EYE"), 4.0)
-    scaled(MB("I8K"), MB("EYE"), 8192.0)
-    scaled(MB("TP1"), MB("TRI"), 4096.0)
-    scaled(MB("NTRI"), MB("TRI"), -4096.0)
+    scaled(MB("TP1"), MB("TRI"), 8192.0)
+    scaled(MB("NTRI"), MB("TRI"), -8192.0)
+    tt(MB("ES2"), MB("SH"), MB("JJ"), ALU.subtract)
+    tt(MB("JI"), MB("JJ"), MB("EYE"), ALU.subtract)
     prep_rest(0)
     scaled(MB("ES1"), MB("SH"), -1.0)
-    scaled(MB("TP2"), MB("TJT"), 4096.0)
-    tt(MB("ES2"), MB("SH"), MB("JJ"), ALU.subtract)
-    tt(MB("IJ"), MB("EYE"), MB("JJ"), ALU.subtract)
+    scaled(MB("TP2"), MB("TJT"), 8192.0)
     tt(MB("EN"), MB("TM1"), MB("TM2"), ALU.subtract)
     ts(all_("sent"), all_("ioi"), col(0), 8192.0, ALU.is_le, ALU.mult)
-    tt(O("ai0", LN, 2 * LN), all_("rin"), O("ai0", 0, LN), ALU.subtract)
     scaled(MB("WT"), MB("BO"), col(4))
 
     def late_constants():
-        scaled(MB("JI"), MB("IJ"), -1.0)
+        scaled(MB("I64"), MB("EYE"), 64.0)
         scaled(MB("N2I"), MB("EYE"), -2.0)
         scaled(O("z8k", 0, 144), O("zz", 0, 144), 8192.0)
         b8 = O("mb", 0, 128, 16)
         scaled(O("pw", 0, 8), b8, col(5))
         scaled(O("pw", 8, 16), b8, col(6))
-        scaled(O("pw", 16, 24), b8, col(7))
-        scaled(O("pw", 24, 32), b8, 1.0)
+        scaled(O("pw", 16, 24), b8, 1.0)
 
     VROWS = RW - SROWS
     for t in range(HO):
@@ -427,7 +423,7 @@ def rank_program(g, core, T, topo):
             gather_tt(O("ad", r0 * LN, r1 * LN), SITE, O("off", r0 * NC, r1 * NC), O("a2", 0, (r1 - r0) * LN), ALU.subtract)
             act(O("ab", r0 * LN, r1 * LN), O("ad", r0 * LN, r1 * LN), ACT.Abs)
             if j == 0:
-                mm(PS(1), MB("C2K"), all_("oneb"), True, False)
+                mm(PS(1), MB("CX"), all_("oneb"), True, False)
                 mm(PS(1), MB("TP1"), osel, False, False)
                 mm(PS(1), MB("TP2"), oselT, False, False)
                 for r in range(VROWS, RW):
@@ -441,14 +437,15 @@ def rank_program(g, core, T, topo):
                 add_rows(VROWS, RW)
                 mm(PS(6), MB("ES1"), osel, True, False)
                 mm(PS(6), MB("ES2"), oselT, False, False)
+            if j == 3:
+                mm(PS(4, 0, LN + LN // 2), MB("EYE"), O("sent", 0, LN + LN // 2), True, False)
         if t == 0:
             late_constants()
         sel = O(so, 0, LN)
-        M, M2 = O(jo, 0, LN), O(jo, LN, 2 * LN)
-        ts(all_("near"), PS(5), O("thr", 0, 1), None, ALU.is_lt)
-        mm(PS(6), MB("EN"), all_("near"), False, True)
-        mm(PS(7), MB("WT"), all_("near"), True, True)
-        mm(PS(4), MB("I8K"), all_("near"), False, True)
+        M, near = O(jo, 0, LN), O(jo, LN, 2 * LN)
+        ts(near, PS(5), O("thr", 0, 1), None, ALU.is_lt)
+        mm(PS(6), MB("EN"), near, False, True)
+        mm(PS(7), MB("WT"), near, True, True)
         ts(sel, PS(6), -0.5, None, ALU.is_lt)
         act(all_("sgn"), PS(7), ACT.Sign, -0.5)
         act(PS(2), all_("sgn"), ACT.Relu, 0.0, -1.0)
@@ -460,20 +457,20 @@ def rank_program(g, core, T, topo):
 
         def v_keep():
             tt(all_("p1"), all_(pi), PS(1), ALU.min)
-            act(all_("xsb"), PS(1), ACT.Copy, -0.5, 1.0 / 4096.0)
 
-        def v_m2():
-            tt(M2, sel, PS(4), ALU.mult)
+        def pe_sites():
             for i in range(RW):
                 mm(PS(3, 0, 2 * NC), Z("zz", i), O(jo, i, 2 * LN, RW), i == 0, i == RW - 1)
 
         def v_sites():
-            cp(O("v16", 0, NC), PS(3, NC, 2 * NC))
-            cp(O("v16", NC, NC + NP), PS(3, NC, 2 * NC, 2))
+            ts(O("h8", 0, NC), PS(3, NC, 2 * NC), 1.0, 8192.0, ALU.min, ALU.mult)
             ts(O("hko", 0, NC), PS(3, 0, NC), 2048.0, None, ALU.add)
 
+        def v_sites2():
+            tt(O("v16", 0, NC), O("h8", 0, NC), PS(3, 0, NC), ALU.add)
+            tt(O("v16", NC, NC + NP), O("h8", 0, NC, 2), PS(3, 0, NC, 2), ALU.add)
+
         def pe_rep():
-            mm(PS(4, 0, LN + LN // 2), MB("EYE"), O("sent", 0, LN + LN // 2), True, False)
             for i in range(RW):
                 mm(PS(4, i, LN + LN // 2, RW), MB("EYE"), O("v16", 0, NC + NP), False, i == RW - 1)
 
@@ -488,8 +485,8 @@ def rank_program(g, core, T, topo):
             mm(PS(5), MB("EYE"), all_("sm"), True, False)
             mm(PS(5), MB("EYE"), O("a2", 0, LN), False, True)
 
-        def v_val():
-            ts(all_("val"), PS(5), 0.5, -0.25, ALU.mult, ALU.add)
+            act(all_("va"), PS(5), ACT.Copy, 127.75, 0.5)
+            act(all_("val"), all_("va"), ACT.Copy, -128.0)
 
         def v_eq():
             tt(O("eq", 0, LN + LN // 2), O("hkk", 0, LN + LN // 2), PS(4, 0, LN + LN // 2), ALU.is_equal)
@@ -503,7 +500,6 @@ def rank_program(g, core, T, topo):
         def v_places():
             tt(O("om", 0, NC), PS(3, 0, NC), O("dum", 0, NC), ALU.min)
             tt(O("o2", 0, NP), PS(3, NC, NC + NP), O("dum", 1, NC, 2), ALU.min)
-            v_val()
             tt(O("om", 1, NC, 2), O("om", 1, NC, 2), O("o2", 0, NP), ALU.max)
             ts(O("ow", 0, NC), O("om", 0, NC), 2048.0, None, ALU.add)
 
@@ -512,18 +508,22 @@ def rank_program(g, core, T, topo):
                 scatter(SITEW, O("ow", 2 * c, 2 * c + 2), O("val", 2 * RW * c, 2 * RW * c + 2 * RW))
 
         def pe_names1():
-            mm(PS(6), MB("NEYE"), all_("xsb"), True, False)
             mm(PS(7), MB("EYE"), all_("p1"), True, False)
-            if last:
-                mm(PS(7), MB("C2K"), all_("oneb"), False, False)
 
         def v_turn_v():
-            tt(all_("xt"), all_("xsb"), PS(2), ALU.mult)
             tt(all_("pt"), all_("p1"), PS(2), ALU.mult)
 
         def pe_names2():
-            mm(PS(6), MB("IJ"), all_("xt"), False, True)
             mm(PS(7), MB("JI"), all_("pt"), False, True)
+            act(PS(6), PS(7), ACT.Relu, -32.0, -1.0 / 64.0)
+            act(all_("gsb"), PS(7), ACT.Relu, -32.0, -1.0 / 64.0)
+
+        def pe_names3():
+            mm(PS(1), MB("EYE"), all_("p1"), True, False)
+            mm(PS(1), MB("JI"), all_("pt"), False, False)
+            if last:
+                mm(PS(1), MB("C2K"), all_("oneb"), False, False)
+            mm(PS(1), MB("I64"), all_("gsb"), False, True)
 
         def v_b1():
             tt(PS(0), all_("sf"), PS(5), ALU.mult)
@@ -534,77 +534,85 @@ def rank_program(g, core, T, topo):
 
         def v_names():
             tt(all_("gb"), all_("bi"), PS(6), ALU.mult)
-            tt(all_("yno") if last else all_(po), all_("gb"), PS(7), ALU.add)
+
+        def v_names2():
+            tt(all_("yno") if last else all_(po), all_("gb"), PS(1), ALU.add)
 
         def v_turned():
             tt(O(so, LN, 2 * LN), sel, PS(2), ALU.mult)
 
         if last:
             r8 = lambda name: O(name, 0, LN, 1, 8)
-            v_m2()
-            v_b1()
+            pe_sites()
             s_hkk()
             v_keep()
             v_sites()
+            v_sites2()
             pe_rep()
             s_new()
-            v_b2()
-            v_eq()
+            v_b1()
             pe_new()
+            v_eq()
             pe_dup()
+            v_turned()
+            v_b2()
             v_turn_v()
-            mm(PS(0, 0, LN, 1, 8), O("pw", 24, 32), M, True, True)
+            mm(PS(0, 0, LN, 1, 8), O("pw", 16, 24), M, True, True)
             act(r8("yso"), PS(0, 0, LN, 1, 8), ACT.Copy, 2048.0)
             dma("y", T.ys[:], ap(r8("yso")), [r8("yso")], [])
             v_places()
+            pe_names1()
+            pe_names2()
+            pe_names3()
+            mm(PS(4, 0, LN, 1, 8), O("pw", 16, 24), O(so, LN, 2 * LN), True, False)
+            for h in range(HO - 1):
+                mm(PS(4, 0, LN, 1, 8), O("pw", 16, 24), O(si, (h + 1) * LN, (h + 2) * LN), False, h == HO - 2)
+            mm(PS(3, 0, LN, 1, 8), O("pw", 0, 8), sel, True, False)
+            mm(PS(3, 0, LN, 1, 8), O("pw", 8, 16), O(so, LN, 2 * LN), False, True)
             v_scatter(NP - 1, -1)
             dma("y", T.yx[:, 0:half], ap(O("xs", 0, half)), [O("xs", 0, half)], [])
             dma("s", T.yx[:, half:SITES], ap(O("xs", half, SITES)), [O("xs", half, SITES)], [])
-            pe_names1()
-            pe_names2()
             v_names()
-            dma("y", T.yn[:], ap(all_("yno")), [all_("yno")], [])
-            v_turned()
-            mm(PS(4, 0, LN, 1, 8), O("pw", 24, 32), O(so, LN, 2 * LN), True, False)
-            for h in range(HO - 1):
-                mm(PS(4, 0, LN, 1, 8), O("pw", 24, 32), O(si, (h + 1) * LN, (h + 2) * LN), False, h == HO - 2)
             cp(r8("yci"), PS(4, 0, LN, 1, 8))
-            mm(PS(6, 0, LN, 1, 8), O("pw", 0, 8), sel, True, False)
-            mm(PS(6, 0, LN, 1, 8), O("pw", 8, 16), O(so, LN, 2 * LN), False, True)
+            v_names2()
+            dma("y", T.yn[:], ap(all_("yno")), [all_("yno")], [])
             ts(r8("ycj"), r8("yci"), 1, None, ALU.bitwise_and)
             ts(r8("ycf"), r8("ycj"), 16.0, None, ALU.mult)
-            tt(r8("ypo"), r8("ycf"), PS(6, 0, LN, 1, 8), ALU.add)
+            tt(r8("ypo"), r8("ycf"), PS(3, 0, LN, 1, 8), ALU.add)
             dma("s", T.yp[:], ap(r8("ypo")), [r8("ypo")], [])
         else:
             v_keep()
-            v_m2()
             pe_names1()
-            v_b1()
-            s_hkk()
             v_turn_v()
             pe_names2()
+            pe_sites()
+            v_b1()
+            s_hkk()
+            pe_names3()
             v_b2()
             v_sites()
+            v_names()
+            v_sites2()
             pe_rep()
             s_new()
-            v_names()
+            v_names2()
             send(all_("pi%d" % (t + 1)), all_(po), "p", t + 1)
+            pe_new()
+            if t == 0:
+                tt(O("ai0", LN, 2 * LN), all_("rin"), O("ai0", 0, LN), ALU.subtract)
             tt(all_("td"), O(ai, LN, 2 * LN), PS(2), ALU.mult)
             mm(PS(0), MB("EYE"), O(ai, 0, LN), True, False)
             mm(PS(0), MB("EYE"), all_("td"), False, True)
             act(O(ao, 0, LN), PS(0), ACT.Copy)
             send(O("ai%d" % (t + 1), 0, LN), O(ao, 0, LN), "a", t + 1)
-            mm(PS(6), MB("BO"), all_("near"), True, True)
-            act(all_("miss"), PS(6), ACT.Relu, 1.0, -1.0, O("cntm", 0, 1))
             v_eq()
             pe_dup()
             v_turned()
-            mm(PS(7, 0, 1), O("m16f", 0, 128), O("cntm", 0, 1), True, True)
             send(O("si%d" % (t + 1), 0, 2 * LN), O(so, 0, 2 * LN), "s", t + 1)
-            pe_new()
-            cp(O("mi", 0, 1), PS(7, 0, 1))
-            ts(O("mi", 1, 2), O("mi", 0, 1), 15, None, ALU.bitwise_and)
-            ts(O("thr", 0, 1), O("mi", 1, 2), 60.0, None, ALU.add)
+            mm(PS(6), MB("BO"), near, True, True)
+            act(all_("miss"), PS(6), ACT.Relu, 1.0, -1.0, O("cntm", 0, 1))
+            prep_site(t + 1)
+            mm(PS(7, 0, 1), O("m16f", 0, 128), O("cntm", 0, 1), True, True)
             mm(PS(1), MB("EYE"), O(ai, LN, 2 * LN), True, False)
             mm(PS(1), MB("N2I"), all_("td"), False, True)
             act(O(ao, LN, 2 * LN), PS(1), ACT.Copy)
@@ -612,7 +620,6 @@ def rank_program(g, core, T, topo):
             if t:
                 send(O("si%d" % (t + 1), 2 * LN, (t + 2) * LN), O(si, LN, (t + 1) * LN), "h", t + 1)
             v_places()
-            prep_site(t + 1)
             c = [NP - 1]
 
             def one_scatter():
@@ -621,6 +628,11 @@ def rank_program(g, core, T, topo):
             for h in range(3):
                 one_scatter()
             prep_lists(t + 1, one_scatter)
-            v_scatter(c[0], -1)
+            one_scatter()
+            cp(O("mi", 0, 1), PS(7, 0, 1))
+            one_scatter()
+            ts(O("mi", 1, 2), O("mi", 0, 1), 15, None, ALU.bitwise_and)
+            one_scatter()
+            ts(O("thr", 0, 1), O("mi", 1, 2), 60.0, None, ALU.add)
             prep_rest(t + 1)
     finish(sent_local[0])

from concourse.mybir import AluOpType, ActivationFunctionType

LN = 320
RW = 16
NC = LN // RW
NP = NC // 2
HO = 4
SITES = 4096
XW = SITES + 448
SROWS = 2

MB_NAMES = ["BO", "TRI", "EYE", "SH", "JJ", "TJ", "TP1", "TP2", "TJT", "NTRI", "EN", "ES1", "ES2", "WT", "NEYE",
            "JI", "I64", "N2I", "CX", "D01", "D10", "Q00", "Q01", "Q10", "Q11", "C2080", "C2K",
            "G8", "TM1", "TM2"]

SCRATCH = {
    "xs": ("sbuf", [128, XW], "bfloat16"),
    "pni": ("sbuf", [128, LN], "int32"),
    "s0i": ("sbuf", [8, LN], "int32"),
    "s0h": ("sbuf", [8, LN], "float16"),
    "kpi": ("sbuf", [128, 1], "int32"),
    "kcol": ("sbuf", [128, 1], "float32"),
    "rin": ("sbuf", [128, LN], "bfloat16"),
    "a2": ("sbuf", [128, 2 * LN], "bfloat16"),
    "ad": ("sbuf", [128, RW * LN], "bfloat16"),
    "ab": ("sbuf", [128, RW * LN], "bfloat16"),
    "off": ("sbuf", [128, LN], "uint16"),
    "mb": ("sbuf", [128, 128 * len(MB_NAMES)], "bfloat16"),
    "zz": ("sbuf", [128, 144], "bfloat16"),
    "z8k": ("sbuf", [128, 144], "bfloat16"),
    "oneb": ("sbuf", [128, LN], "bfloat16"),
    "neg": ("sbuf", [128, NP], "bfloat16"),
    "ioi": ("sbuf", [128, LN], "float32"),
    "sent": ("sbuf", [128, LN + LN // 2], "bfloat16"),
    "pidx": ("sbuf", [128, 4], "int32"),
    "cols": ("sbuf", [128, 16], "float32"),
    "pw": ("sbuf", [128, 32], "bfloat16"),
    "dum": ("sbuf", [128, NC], "float32"),
    "m16f": ("sbuf", [128, 128], "float32"),
    "thr": ("sbuf", [128, 1], "float32"),
    "mi": ("sbuf", [128, 2], "int32"),
    "cntm": ("sbuf", [128, 1], "float32"),
    "sf": ("sbuf", [128, LN], "float32"),
    "w2": ("sbuf", [128, LN], "float32"),
    "wk": ("sbuf", [128, LN], "float32"),
    "zi": ("sbuf", [128, LN], "int32"),
    "hi": ("sbuf", [128, LN], "int32"),
    "hc": ("sbuf", [128, LN], "float16"),
    "th": ("sbuf", [128, LN], "float16"),
    "miss": ("sbuf", [128, LN], "bfloat16"),
    "sgn": ("sbuf", [128, LN], "float32"),
    "q2": ("sbuf", [128, LN], "int32"),
    "bi": ("sbuf", [128, LN], "int32"),
    "p1": ("sbuf", [128, LN], "float16"),
    "pt": ("sbuf", [128, LN], "float16"),
    "gsb": ("sbuf", [128, LN], "bfloat16"),
    "gb": ("sbuf", [128, LN], "float32"),
    "td": ("sbuf", [128, LN], "bfloat16"),
    "hkk": ("sbuf", [128, LN + LN // 2], "float32"),
    "hko": ("sbuf", [128, NC], "uint16"),
    "v16": ("sbuf", [128, NC + NP], "float16"),
    "eq": ("sbuf", [128, LN + LN // 2], "bfloat16"),
    "om": ("sbuf", [128, NC], "float32"),
    "o2": ("sbuf", [128, NP], "float32"),
    "ow": ("sbuf", [128, NC], "uint16"),
    "sm": ("sbuf", [128, LN], "bfloat16"),
    "va": ("sbuf", [128, LN], "bfloat16"),
    "val": ("sbuf", [128, LN], "bfloat16"),
    "h8": ("sbuf", [128, NC], "float16"),
    "yno": ("sbuf", [128, LN], "float32"),
    "yso": ("sbuf", [8, LN], "float32"),
    "yci": ("sbuf", [8, LN], "int32"),
    "ycj": ("sbuf", [8, LN], "int32"),
    "ycf": ("sbuf", [8, LN], "float32"),
    "ypo": ("sbuf", [8, LN], "float32"),
}
for _t in range(HO + 1):
    SCRATCH["si%d" % _t] = ("sbuf", [128, 4 * LN], "bfloat16")
    SCRATCH["ai%d" % _t] = ("sbuf", [128, 2 * LN], "bfloat16")
    SCRATCH["pi%d" % _t] = ("sbuf", [128, LN], "float16")
    SCRATCH["ji%d" % _t] = ("sbuf", [128, LN], "float16")
for _t in range(1, HO + 1):
    SCRATCH["so%d" % _t] = ("sbuf", [128, 2 * LN], "bfloat16")
    SCRATCH["ao%d" % _t] = ("sbuf", [128, 2 * LN], "bfloat16")
    SCRATCH["po%d" % _t] = ("sbuf", [128, LN], "float16")
    SCRATCH["jo%d" % _t] = ("sbuf", [128, 2 * LN], "float16")
for _k in ("si4", "ai4", "pi4", "ji0", "ji4"):
    del SCRATCH[_k]
for _k in range(8):
    SCRATCH["ps%d" % _k] = ("psum", [128, 16, 32] if _k == 5 else [128, 512], "float32")

NDMA = 16
SEMAPHORES = (["eV", "eS", "eT", "eG", "ls"] + ["d%d" % i for i in range(NDMA)]
              + ["r%s%d" % (k, t) for t in range(1, HO) for k in "japshd"])


def O(name, a, b, step=1, p=None):
    return (name, a, b, step, p)


def make_queue(g, T):
    eng = {"v": g.vector, "s": g.scalar, "t": g.tensor, "g": g, "y": g.sync}
    esem = {"v": "eV", "s": "eS", "t": "eT", "g": "eG"}
    know = {q: {} for q in eng}
    count = {}
    snaps = {}
    recs = {}

    def learn(q, tok):
        k = know[q]
        if k.get(tok[0], 0) >= tok[1]:
            return
        eng[q].wait_ge(T.sem[tok[0]], tok[1])
        k[tok[0]] = tok[1]
        for s, n in snaps.get(tok, {}).items():
            if k.get(s, 0) < n:
                k[s] = n

    def ap(o):
        name, a, b, step, p = o
        t = T[name]
        if name == "ps5":
            return t[:, 0:NP, :] if p is None else t[:, 0:NP, p[0]:p[1]]
        if p is None:
            return t[:, a:b] if step == 1 else t[:, a:b:step]
        return t[0:p, a:b] if step == 1 else t[0:p, a:b:step]

    def needs(q, tag, reads, writes):
        out = []
        for lst, w in ((reads, False), (writes, True)):
            for o in lst:
                ps = o[0].startswith("ps")
                for (a, b, step, rw, rq, tok) in recs.get(o[0], []):
                    if not ps and (a >= o[2] or b <= o[1]):
                        continue
                    if not ps and step == o[3] and step > 1 and (a - o[1]) % step:
                        continue
                    if rq == tag and tag != "dma":
                        if (rw or w) and not (w and tag == "t"):
                            out.append(tok)
                        continue
                    if w or rw or ps:
                        out.append(tok)
        return out

    def note(tag, tok, reads, writes):
        for lst, w in ((reads, False), (writes, True)):
            for o in lst:
                ps = o[0].startswith("ps")
                a, b, st = (0, 1 << 20, 1) if ps else (o[1], o[2], o[3])
                old = recs.get(o[0], [])
                if w:
                    old = [r for r in old if not (r[0] >= a and r[1] <= b and st == 1)]
                elif tag != "dma":
                    old = [r for r in old if not (r[0] >= a and r[1] <= b and st == 1 and not r[3] and r[4] == tag)]
                recs[o[0]] = old + [(a, b, st, w, tag, tok)]

    def op(q, fn, reads, writes):
        need = needs(q, q, reads, writes)
        for tok in sorted(set(need), key=lambda x: -x[1]):
            learn(q, tok)
        s = esem[q]
        count[s] = count.get(s, 0) + 1
        fn().then_inc(T.sem[s], 1)
        tok = (s, count[s])
        snaps[tok] = dict(know[q])
        note(q, tok, reads, writes)
        return tok

    ndma = [0]

    def dma(q, out, in_, reads, writes):
        for tok in set(needs(q, "dma", reads, writes)):
            learn(q, tok)
        s = "d%d" % ndma[0]
        ndma[0] += 1
        eng[q].dma_start(out, in_).then_inc(T.sem[s], 16)
        tok = (s, 16)
        count[s] = 16
        snaps[tok] = dict(know[q])
        note("dma", tok, reads, writes)

    def arrive(s, n, o):
        tok = (s, n)
        count[s] = n
        note("dma", tok, [], [o])

    def ready(q, reads):
        for tok in sorted(set(needs(q, "dma", reads, [])), key=lambda x: -x[1]):
            learn(q, tok)

    def finish(local):
        for s, n in sorted(count.items()):
            learn("g", (s, n))
        if local:
            g.wait_ge(T.sem.ls, local)

    return ap, op, dma, arrive, ready, finish


def rank_program(g, core, T, topo):
    rank = T.rank_of(core)
    if rank is None:
        return
    n = len(T.cores)
    nxt, prv = T.cores[(rank + 1) % n], T.cores[(rank - 1) % n]
    ap, op, dma, arrive, ready, finish = make_queue(g, T)
    ALU, ACT = AluOpType, ActivationFunctionType
    V, S, PE = g.vector, g.scalar, g.tensor

    def tt(out, i0, i1, f):
        op("v", lambda: V.tensor_tensor(ap(out), ap(i0), ap(i1), f), [i0, i1], [out])

    def ts(out, i0, s1, s2, f0, f1=None):
        cols = [x for x in (s1, s2) if isinstance(x, tuple)]
        a1 = ap(s1) if isinstance(s1, tuple) else s1
        a2 = ap(s2) if isinstance(s2, tuple) else s2
        if f1 is None:
            op("v", lambda: V.tensor_scalar(ap(out), ap(i0), a1, None, f0), [i0] + cols, [out])
        else:
            op("v", lambda: V.tensor_scalar(ap(out), ap(i0), a1, a2, f0, f1), [i0] + cols, [out])

    def cp(out, i0):
        op("v", lambda: V.tensor_copy(ap(out), ap(i0)), [i0], [out])

    def fill(out, c):
        op("v", lambda: V.memset(ap(out), c), [], [out])

    def act(out, i0, f, bias=0.0, scale=1.0, acc=None):
        rd = [i0] + [x for x in (bias, scale) if isinstance(x, tuple)]
        bb = ap(bias) if isinstance(bias, tuple) else bias
        ss = ap(scale) if isinstance(scale, tuple) else scale
        if acc is None:
            op("s", lambda: S.activation(ap(out), ap(i0), f, bias=bb, scale=ss), rd, [out])
        else:
            op("s", lambda: S.activation(ap(out), ap(i0), f, bias=bb, scale=ss, accum_out=ap(acc)), rd, [out, acc])

    def scaled(out, i0, c):
        act(out, i0, ACT.Identity, 0.0, c)

    def mm(out, lhsT, rhs, start, stop):
        op("t", lambda: PE.matmul(ap(out), ap(lhsT), ap(rhs), start, stop), [lhsT, rhs], [out])

    def aff(out, i0, pattern, cmp_, base, cm):
        op("g", lambda: g.affine_select(ap(out), ap(i0), pattern, cmp_, 0.0, base, cm), [i0], [out])

    def iota(out, pattern, base, cm):
        op("g", lambda: g.iota(ap(out), pattern, base, cm, allow_small_or_imprecise_dtypes=True), [], [out])

    def gather_tt(out, win, offs, i1, f):
        op("v", lambda: V.tensor_tensor(ap(out), ap(win).indirect(ap(offs)), ap(i1), f), [win, offs, i1], [out])

    def gather_act(out, win, offs):
        op("s", lambda: S.activation(ap(out), ap(win).indirect(ap(offs)), ACT.Copy), [win, offs], [out])

    def scatter(win, offs, i0):
        op("v", lambda: V.tensor_copy(ap(win).indirect(ap(offs)), ap(i0)), [i0, offs], [win])

    sent_local = [0]

    def send(dst, src, key, t):
        ready("g", [src])
        rid, pid, _ = topo.addr(nxt)
        g.remote_dma(ap(dst), ap(src), T.sem["r%s%d" % (key, t)], T.sem.ls, pid, rid, topo.mask(core, nxt))
        sent_local[0] += len(topo.engines(core, nxt))

    def MB(k, p=None):
        i = MB_NAMES.index(k)
        return O("mb", 128 * i, 128 * i + 128, 1, p)

    def Z(name, k):
        return O(name, 15 - k, 143 - k)

    def PS(k, a=0, b=LN, step=1, p=None):
        return O("ps%d" % k, a, b, step, p)

    def all_(name):
        return O(name, 0, LN)

    SITE = O("xs", 0, SITES)
    SITEW = O("xs", 0, XW)
    half = SITES // 2

    dma("y", ap(all_("pni")), T.pn[:], [], [all_("pni")])
    dma("s", ap(all_("s0i")), T.s0[:], [], [all_("s0i")])
    dma("s", ap(O("kpi", 0, 1)), T.kap[:], [], [O("kpi", 0, 1)])
    dma("y", ap(O("ai0", 0, LN)), T.a0[:], [], [O("ai0", 0, LN)])
    dma("y", ap(O("xs", 0, half)), T.x[:, 0:half], [], [O("xs", 0, half)])
    dma("s", ap(O("xs", half, SITES)), T.x[:, half:SITES], [], [O("xs", half, SITES)])
    dma("y", ap(all_("rin")), T.r0[:], [], [all_("rin")])

    for t in range(1, HO):
        k = len(topo.engines(prv, core))
        arrive("rj%d" % t, k, all_("ji%d" % t))
        arrive("ra%d" % t, k, O("ai%d" % t, 0, LN))
        arrive("rd%d" % t, k, O("ai%d" % t, LN, 2 * LN))
        arrive("rp%d" % t, k, all_("pi%d" % t))
        arrive("rs%d" % t, k, O("si%d" % t, 0, 2 * LN))
        if t > 1:
            arrive("rh%d" % t, k, O("si%d" % t, 2 * LN, (t + 1) * LN))

    op("g", lambda: g.iota(ap(O("pidx", 0, 1)), [[0, 1]], 0, 1), [], [O("pidx", 0, 1)])
    fill(all_("oneb"), 1.0)
    fill(MB("C2080"), 16.25)
    one = O("oneb", 0, 128)
    one8 = O("oneb", 0, 128, 1, 8)
    aff(MB("TM1", 8), one8, [[1, 128]], ALU.is_ge, 0, -16)
    aff(MB("G8", 8), MB("TM1", 8), [[-1, 128]], ALU.is_ge, 15, 16)
    aff(MB("EYE"), one, [[-1, 128]], ALU.is_equal, 0, 1)
    aff(MB("D01"), one, [[1, 128]], ALU.is_equal, -16, -1)
    aff(MB("D10"), one, [[1, 128]], ALU.is_equal, 16, -1)
    aff(MB("TM2"), one, [[-16, 8], [0, 16]], ALU.is_ge, 0, 1)
    aff(MB("BO"), MB("TM2"), [[16, 8], [0, 16]], ALU.is_ge, 15, -1)
    aff(MB("TRI"), MB("BO"), [[-1, 128]], ALU.is_ge, 0, 1)
    aff(MB("TJ"), MB("BO"), [[16, 8], [-1, 16]], ALU.is_ge, 14, -1)
    aff(MB("JJ"), one, [[-16, 8], [1, 16]], ALU.is_equal, -15, 1)
    aff(MB("SH"), MB("BO"), [[1, 128]], ALU.is_equal, -1, -1)
    iota(O("dum", 0, NC), [[16, NC]], 2048, 1)
    iota(all_("ioi"), [[0, NC], [1, RW]], 0, 0)

    def col(i):
        return O("cols", i, i + 1)
    ts(O("pidx", 1, 2), O("pidx", 0, 1), 15, None, ALU.bitwise_and)
    ts(O("pidx", 2, 3), O("pidx", 0, 1), 4, 1, ALU.arith_shift_right, ALU.bitwise_and)
    cp(col(0), O("pidx", 1, 2))
    cp(col(2), O("pidx", 2, 3))
    ts(col(3), col(2), -1.0, 1.0, ALU.mult, ALU.add)
    ts(col(1), col(0), 15.0, None, ALU.is_equal)
    ts(col(5), col(0), 1.0, None, ALU.add)
    ts(col(6), col(0), -2.0, 14.0, ALU.mult, ALU.add)
    fill(O("zz", 0, 144), 0.0)
    fill(MB("CX"), (8192.0 - 2112.0) / 128.0)
    fill(MB("C2K"), 16.0)
    fill(O("thr", 0, 1), 60.0)
    fill(O("m16f", 0, 128), 1.0 / 16.0)
    fill(O("neg", 0, NP), -4096.0)
    fill(O("sent", LN, LN + LN // 2), 0.0)
    ts(col(4), col(1), -101.0, 1.0, ALU.mult, ALU.add)
    ts(O("si0", 0, LN), all_("oneb"), col(1), None, ALU.mult)
    ts(O("si0", LN, 2 * LN), all_("oneb"), col(1), None, ALU.mult)
    ts(O("s0h", 0, LN, 1, 8), O("s0i", 0, LN, 1, 8), -2048.0, None, ALU.add)
    ts(O("kcol", 0, 1), O("kpi", 0, 1), 32.0, -37888.0 - 80.0 * 131072.0, ALU.mult, ALU.add)
    ts(all_("pi0"), all_("pni"), -2048.0, None, ALU.add)

    def prep_site(t):
        if t == 0:
            mm(PS(0), MB("G8", 8), O("s0h", 0, LN, 1, 8), True, False)
        else:
            mm(PS(0), MB("BO"), all_("ji%d" % t), True, False)
        mm(PS(0), MB("C2080"), all_("oneb"), False, True)
        act(all_("wk"), PS(0), ACT.Identity, O("kcol", 0, 1), 3232.0)

    def prep_lists(t, between=lambda: None):
        tt(PS(6), all_("pi%d" % t), PS(0), ALU.mult)
        between()
        act(all_("sf"), PS(0), ACT.Copy, -32.0)
        act(all_("w2"), PS(0), ACT.Copy, -32.0 * 2080.0 + 32.0 * 811.0 * t - 8388608.0, 2080.0)
        tt(all_("zi"), all_("wk"), PS(6), ALU.add)
        between()
        ts(all_("hi"), all_("zi"), 5, SITES - 1, ALU.arith_shift_right, ALU.bitwise_and)
        between()
        ts(all_("hc"), all_("hi"), -2048.0, None, ALU.add)
        between()
        for b in range(NP):
            o, i = O("th", b, LN, NP), O("hc", 32 * b, 32 * b + 32)
            op("v", lambda: V.transpose(ap(o), ap(i)), [i], [o])
        for x in range(2):
            for y2 in range(2):
                mm(PS(2, x, LN, 2), MB("Q%d%d" % (x, y2)), O("th", 160 * y2, 160 * y2 + 160), y2 == 0, y2 == 1)
        mm(PS(3), MB("EYE"), all_("hc"), True, True)

    def prep_rest(t):
        ts(all_("off"), PS(2), 2048.0, None, ALU.add)
        act(O("a2", 0, LN), O("ai%d" % t, 0, LN), ACT.Copy)
        act(O("a2", LN, 2 * LN), O("ai%d" % t, 0, LN), ACT.Copy)

    scaled(MB("Q00"), MB("EYE"), col(3))
    scaled(MB("Q11"), MB("EYE"), col(2))
    scaled(MB("Q01"), MB("D01"), col(3))
    scaled(MB("Q10"), MB("D10"), col(2))
    prep_site(0)
    prep_lists(0)
    cp(O("zz", 15, 143, 16), O("mb", 0, 128, 16))
    tt(MB("TJT"), MB("TJ"), MB("TRI"), ALU.subtract)
    scaled(MB("NEYE"), MB("EYE"), -1.0)
    scaled(MB("TM1"), MB("TRI"), 3.0)
    scaled(MB("TM2"), MB("EYE"), 4.0)
    scaled(MB("TP1"), MB("TRI"), 8192.0)
    scaled(MB("NTRI"), MB("TRI"), -8192.0)
    tt(MB("ES2"), MB("SH"), MB("JJ"), ALU.subtract)
    tt(MB("JI"), MB("JJ"), MB("EYE"), ALU.subtract)
    prep_rest(0)
    scaled(MB("ES1"), MB("SH"), -1.0)
    scaled(MB("TP2"), MB("TJT"), 8192.0)
    tt(MB("EN"), MB("TM1"), MB("TM2"), ALU.subtract)
    ts(all_("sent"), all_("ioi"), col(0), 8192.0, ALU.is_le, ALU.mult)
    scaled(MB("WT"), MB("BO"), col(4))

    def late_constants():
        scaled(MB("I64"), MB("EYE"), 64.0)
        scaled(MB("N2I"), MB("EYE"), -2.0)
        scaled(O("z8k", 0, 144), O("zz", 0, 144), 8192.0)
        b8 = O("mb", 0, 128, 16)
        scaled(O("pw", 0, 8), b8, col(5))
        scaled(O("pw", 8, 16), b8, col(6))
        scaled(O("pw", 16, 24), b8, 1.0)

    VROWS = RW - SROWS
    for t in range(HO):
        last = t == HO - 1
        si, ai, pi = "si%d" % t, "ai%d" % t, "pi%d" % t
        so, ao, po, jo = "so%d" % (t + 1), "ao%d" % (t + 1), "po%d" % (t + 1), "jo%d" % (t + 1)
        osel, oselT = O(si, 0, LN), O(si, LN, 2 * LN)
        mm(PS(5), MB("TP1"), osel, True, False)
        mm(PS(5), MB("TP2"), oselT, False, False)
        gather_act(O("ad", VROWS * LN, RW * LN), SITE, O("off", VROWS * NC, RW * NC))

        def add_rows(r0, r1):
            for r in range(r0, r1):
                mm(PS(5), Z("zz", r), O("ab", r * LN, r * LN + LN), False, r == VROWS - 1)
        steps = [(k, k + 2) for k in range(0, VROWS - 2, 2)] + [(VROWS - 2, VROWS - 1), (VROWS - 1, VROWS)]
        for j, (r0, r1) in enumerate(steps):
            gather_tt(O("ad", r0 * LN, r1 * LN), SITE, O("off", r0 * NC, r1 * NC), O("a2", 0, (r1 - r0) * LN), ALU.subtract)
            act(O("ab", r0 * LN, r1 * LN), O("ad", r0 * LN, r1 * LN), ACT.Abs)
            if j == 0:
                mm(PS(1), MB("CX"), all_("oneb"), True, False)
                mm(PS(1), MB("TP1"), osel, False, False)
                mm(PS(1), MB("TP2"), oselT, False, False)
                for r in range(VROWS, RW):
                    bank = 6 + r - VROWS
                    mm(PS(bank), MB("EYE"), O("ad", r * LN, r * LN + LN), True, False)
                    mm(PS(bank), MB("NEYE"), O("a2", 0, LN), False, True)
            add_rows(r0, r1)
            if j == 2:
                for r in range(VROWS, RW):
                    act(O("ab", r * LN, r * LN + LN), PS(6 + r - VROWS), ACT.Abs)
                add_rows(VROWS, RW)
                mm(PS(6), MB("ES1"), osel, True, False)
                mm(PS(6), MB("ES2"), oselT, False, False)
            if j == 3:
                mm(PS(4, 0, LN + LN // 2), MB("EYE"), O("sent", 0, LN + LN // 2), True, False)
        if t == 0:
            late_constants()
        sel = O(so, 0, LN)
        M, near = O(jo, 0, LN), O(jo, LN, 2 * LN)
        ts(near, PS(5), O("thr", 0, 1), None, ALU.is_lt)
        mm(PS(6), MB("EN"), near, False, True)
        mm(PS(7), MB("WT"), near, True, True)
        ts(sel, PS(6), -0.5, None, ALU.is_lt)
        act(all_("sgn"), PS(7), ACT.Sign, -0.5)
        act(PS(2), all_("sgn"), ACT.Relu, 0.0, -1.0)
        tt(M, sel, PS(3), ALU.mult)
        mm(PS(1), MB("NTRI"), sel, False, True)
        mm(PS(5), MB("BO"), M, True, True)
        if not last:
            send(all_("ji%d" % (t + 1)), M, "j", t + 1)

        def v_keep():
            tt(all_("p1"), all_(pi), PS(1), ALU.min)

        def pe_sites():
            for i in range(RW):
                mm(PS(3, 0, 2 * NC), Z("zz", i), O(jo, i, 2 * LN, RW), i == 0, i == RW - 1)

        def v_sites():
            ts(O("h8", 0, NC), PS(3, NC, 2 * NC), 1.0, 8192.0, ALU.min, ALU.mult)
            ts(O("hko", 0, NC), PS(3, 0, NC), 2048.0, None, ALU.add)

        def v_sites2():
            tt(O("v16", 0, NC), O("h8", 0, NC), PS(3, 0, NC), ALU.add)
            tt(O("v16", NC, NC + NP), O("h8", 0, NC, 2), PS(3, 0, NC, 2), ALU.add)

        def pe_rep():
            for i in range(RW):
                mm(PS(4, i, LN + LN // 2, RW), MB("EYE"), O("v16", 0, NC + NP), False, i == RW - 1)

        def s_hkk():
            act(all_("hkk"), PS(5), ACT.Copy)
            act(O("hkk", LN, LN + LN // 2), PS(5, 0, LN, 1, (16, 32)), ACT.Copy)

        def s_new():
            gather_act(all_("sm"), SITE, O("hko", 0, NC))

        def pe_new():
            mm(PS(5), MB("EYE"), all_("sm"), True, False)
            mm(PS(5), MB("EYE"), O("a2", 0, LN), False, True)

            act(all_("va"), PS(5), ACT.Copy, 127.75, 0.5)
            act(all_("val"), all_("va"), ACT.Copy, -128.0)

        def v_eq():
            tt(O("eq", 0, LN + LN // 2), O("hkk", 0, LN + LN // 2), PS(4, 0, LN + LN // 2), ALU.is_equal)

        def pe_dup():
            for i in range(RW):
                mm(PS(3, 0, NC + NP), Z("z8k", i), O("eq", i, LN + LN // 2, RW), i == 0, False)
            mm(PS(3, 0, NC), MB("EYE"), O("v16", 0, NC), False, False)
            mm(PS(3, NC, NC + NP), MB("EYE"), O("neg", 0, NP), False, True)

        def v_places():
            tt(O("om", 0, NC), PS(3, 0, NC), O("dum", 0, NC), ALU.min)
            tt(O("o2", 0, NP), PS(3, NC, NC + NP), O("dum", 1, NC, 2), ALU.min)
            tt(O("om", 1, NC, 2), O("om", 1, NC, 2), O("o2", 0, NP), ALU.max)
            ts(O("ow", 0, NC), O("om", 0, NC), 2048.0, None, ALU.add)

        def v_scatter(c0, c1):
            for c in range(c0, c1, -1):
                scatter(SITEW, O("ow", 2 * c, 2 * c + 2), O("val", 2 * RW * c, 2 * RW * c + 2 * RW))

        def pe_names1():
            mm(PS(7), MB("EYE"), all_("p1"), True, False)

        def v_turn_v():
            tt(all_("pt"), all_("p1"), PS(2), ALU.mult)

        def pe_names2():
            mm(PS(7), MB("JI"), all_("pt"), False, True)
            act(PS(6), PS(7), ACT.Relu, -32.0, -1.0 / 64.0)
            act(all_("gsb"), PS(7), ACT.Relu, -32.0, -1.0 / 64.0)

        def pe_names3():
            mm(PS(1), MB("EYE"), all_("p1"), True, False)
            mm(PS(1), MB("JI"), all_("pt"), False, False)
            if last:
                mm(PS(1), MB("C2K"), all_("oneb"), False, False)
            mm(PS(1), MB("I64"), all_("gsb"), False, True)

        def v_b1():
            tt(PS(0), all_("sf"), PS(5), ALU.mult)

        def v_b2():
            tt(all_("q2"), all_("w2"), PS(0), ALU.add)
            ts(all_("bi"), all_("q2"), 5, SITES - 1, ALU.arith_shift_right, ALU.bitwise_and)

        def v_names():
            tt(all_("gb"), all_("bi"), PS(6), ALU.mult)

        def v_names2():
            tt(all_("yno") if last else all_(po), all_("gb"), PS(1), ALU.add)

        def v_turned():
            tt(O(so, LN, 2 * LN), sel, PS(2), ALU.mult)

        if last:
            r8 = lambda name: O(name, 0, LN, 1, 8)
            pe_sites()
            s_hkk()
            v_keep()
            v_sites()
            v_sites2()
            pe_rep()
            s_new()
            v_b1()
            pe_new()
            v_eq()
            pe_dup()
            v_turned()
            v_b2()
            v_turn_v()
            mm(PS(0, 0, LN, 1, 8), O("pw", 16, 24), M, True, True)
            act(r8("yso"), PS(0, 0, LN, 1, 8), ACT.Copy, 2048.0)
            dma("y", T.ys[:], ap(r8("yso")), [r8("yso")], [])
            v_places()
            pe_names1()
            pe_names2()
            pe_names3()
            mm(PS(4, 0, LN, 1, 8), O("pw", 16, 24), O(so, LN, 2 * LN), True, False)
            for h in range(HO - 1):
                mm(PS(4, 0, LN, 1, 8), O("pw", 16, 24), O(si, (h + 1) * LN, (h + 2) * LN), False, h == HO - 2)
            mm(PS(3, 0, LN, 1, 8), O("pw", 0, 8), sel, True, False)
            mm(PS(3, 0, LN, 1, 8), O("pw", 8, 16), O(so, LN, 2 * LN), False, True)
            v_scatter(NP - 1, -1)
            dma("y", T.yx[:, 0:half], ap(O("xs", 0, half)), [O("xs", 0, half)], [])
            dma("s", T.yx[:, half:SITES], ap(O("xs", half, SITES)), [O("xs", half, SITES)], [])
            v_names()
            cp(r8("yci"), PS(4, 0, LN, 1, 8))
            v_names2()
            dma("y", T.yn[:], ap(all_("yno")), [all_("yno")], [])
            ts(r8("ycj"), r8("yci"), 1, None, ALU.bitwise_and)
            ts(r8("ycf"), r8("ycj"), 16.0, None, ALU.mult)
            tt(r8("ypo"), r8("ycf"), PS(3, 0, LN, 1, 8), ALU.add)
            dma("s", T.yp[:], ap(r8("ypo")), [r8("ypo")], [])
        else:
            v_keep()
            pe_names1()
            v_turn_v()
            pe_names2()
            pe_sites()
            v_b1()
            s_hkk()
            pe_names3()
            v_b2()
            v_sites()
            v_names()
            v_sites2()
            pe_rep()
            s_new()
            v_names2()
            send(all_("pi%d" % (t + 1)), all_(po), "p", t + 1)
            pe_new()
            if t == 0:
                tt(O("ai0", LN, 2 * LN), all_("rin"), O("ai0", 0, LN), ALU.subtract)
            tt(all_("td"), O(ai, LN, 2 * LN), PS(2), ALU.mult)
            mm(PS(0), MB("EYE"), O(ai, 0, LN), True, False)
            mm(PS(0), MB("EYE"), all_("td"), False, True)
            act(O(ao, 0, LN), PS(0), ACT.Copy)
            send(O("ai%d" % (t + 1), 0, LN), O(ao, 0, LN), "a", t + 1)
            v_eq()
            pe_dup()
            v_turned()
            send(O("si%d" % (t + 1), 0, 2 * LN), O(so, 0, 2 * LN), "s", t + 1)
            mm(PS(6), MB("BO"), near, True, True)
            act(all_("miss"), PS(6), ACT.Relu, 1.0, -1.0, O("cntm", 0, 1))
            prep_site(t + 1)
            mm(PS(7, 0, 1), O("m16f", 0, 128), O("cntm", 0, 1), True, True)
            mm(PS(1), MB("EYE"), O(ai, LN, 2 * LN), True, False)
            mm(PS(1), MB("N2I"), all_("td"), False, True)
            act(O(ao, LN, 2 * LN), PS(1), ACT.Copy)
            send(O("ai%d" % (t + 1), LN, 2 * LN), O(ao, LN, 2 * LN), "d", t + 1)
            if t:
                send(O("si%d" % (t + 1), 2 * LN, (t + 2) * LN), O(si, LN, (t + 1) * LN), "h", t + 1)
            v_places()
            c = [NP - 1]

            def one_scatter():
                v_scatter(c[0], c[0] - 1)
                c[0] -= 1
            for h in range(3):
                one_scatter()
            prep_lists(t + 1, one_scatter)
            one_scatter()
            cp(O("mi", 0, 1), PS(7, 0, 1))
            one_scatter()
            ts(O("mi", 1, 2), O("mi", 0, 1), 15, None, ALU.bitwise_and)
            one_scatter()
            ts(O("thr", 0, 1), O("mi", 1, 2), 60.0, None, ALU.add)
            prep_rest(t + 1)
    finish(sent_local[0])
